import numpy as np, ml_dtypes
CORES = [16,18,20,22]
N = 4
BF = ml_dtypes.bfloat16
def f(rng, *shape):
    return (rng.standard_normal(shape, dtype=np.float32) * np.exp2(rng.integers(-2, 3, shape[:-1] + (1,)))).astype(BF)
def wide(rng, *shape):
    v = f(rng, *shape).astype(np.float32); k = shape[:-2] + (1, shape[-1])
    return (v * np.exp2(rng.integers(-6, 7, k)) * (rng.random(k) > 0.0625)).astype(BF)
M, K, TR, CAP = 4096, 64, 4, 384
D = 16 * K
def hashes(s, n):
    lo = ((s & 4095) + 1597 * n) & 4095; b = ((s >> 12) + ((lo * lo) >> 6)) & 4095
    return (lo + ((b * b) >> 6)) & 4095, b
def seed_of(a, b, n):
    lo = (a - ((b * b) >> 6)) & 4095
    return ((b - ((lo * lo) >> 6)) & 4095) * 4096 + ((lo - 1597 * n) & 4095)
def owners(t, s):
    a, b = hashes(np.asarray(s, np.int64)[..., None], (TR + 1) * np.arange(K)); w = (a * N) >> 12
    return np.where(b < t[w], w, t[N + w]).astype(np.int64)
def loads(t, s):
    o = owners(t, s); return np.stack([np.sum(o == q, -1) for q in range(N)], -1)
def sixteen(rng, t, keep=()):
    m = 16 - len(keep); kept = np.array(keep, np.int64); base = np.sum(loads(t, kept), 0)
    pool = rng.integers(0, 1 << 24, 1024); c = loads(t, pool); ok = np.flatnonzero(np.all(c * m <= CAP - base, 1)); j = np.arange(m)
    for u in range(m):
        if np.all(np.sum(c[j], 0) + base <= CAP): break
        j[u] = rng.choice(ok)
    return rng.permutation(np.concatenate([pool[j], kept]))
def ranks(rng, least):
    return np.concatenate([rng.integers(least, 4097, N), rng.permutation(N)]).astype(np.int64)
def absent(rng):
    w = rng.permutation(N); t = np.zeros(2 * N, np.int64)
    t[w] = (8192 * np.arange(N) + N - 1) // (2 * (N - 1)); t[N + w] = np.roll(w, -1); return t
def history(rng, dens):
    w = np.zeros((N, 128, M), np.float32)
    for q in range(N):
        for r in range(N):
            w[q] += np.float32(2 ** r) * (rng.random((128, M), dtype=np.float32) < dens[r][:, None])
    return w.astype(BF)
def seeds(rng, rk):
    return np.stack([np.stack([sixteen(rng, rk[g]) for g in range(8)]) for r in range(N)])
def complete(rng, rk, sd, dens=None):
    if dens is None: dens = rng.choice(np.array([0.1, 0.5, 0.9]), (N, 128))
    return {"sd": np.reshape(sd, (N, 128, 1)).astype(np.int32), "rk": np.stack([rk] * N).astype(np.int32), "thr": rng.integers(0, 4097, (N, 8, M)).astype(np.int32),
            "ali": rng.integers(0, M, (N, 8, M)).astype(np.int32), "seen": history(rng, dens), "vec": f(rng, N, 128, M)}
def setup_inputs(rng):
    rk = np.stack([ranks(rng, 2800) for g in range(8)]); return complete(rng, rk, seeds(rng, rk))
def setup_inputs_full(rng):
    o0 = rng.integers(0, N); rk = []
    for g in range(8):
        o = (o0 + g) % N; t = np.concatenate([rng.integers(3577 - 40, 3577 + 41, N), np.full(N, o)]).astype(np.int64); t[o] = 4096; rk.append(t)
    rk = np.stack(rk); sd = seeds(rng, rk); C = CAP // 16
    far = rng.integers(0, N, 8); h = rng.permutation(8); far[h[0]] = 0; far[h[1]] = rng.integers(1, N)
    for g in range(8):
        o = (o0 + g) % N; r = (o + far[g]) % N
        pool = rng.integers(0, 1 << 24, 4096); c = loads(rk[g], pool); fine = np.all(np.delete(c, o, 1) <= C, 1); s = []
        for i in range(8):
            x = rng.integers(-2, 3)
            for v in (C + x, C - x): s.append(pool[rng.choice(np.flatnonzero(fine & (c[:, o] == v)))])
        sd[r, g] = rng.permutation(np.array(s))
    return complete(rng, rk, sd)
def setup_inputs_edges(rng):
    rk, tie = [], []
    for g in range(8):
        t = ranks(rng, 3500); w = rng.permutation(N)[:4]; t[w[0]] = 0; t[N + w[0]] = w[1]; t[w[1]] = 0; t[N + w[1]] = w[0]; t[w[2]] = rng.integers(3500, 4096); t[N + w[2]] = w[0]; t[w[3]] = 4096; rk.append(t)
        tie.append(seed_of(int(w[2]) * (4096 // N) + int(rng.integers(0, 4096 // N)), int(t[w[2]]), (TR + 1) * int(rng.integers(0, K))))
    rk = np.stack(rk); sd = np.stack([np.stack([sixteen(rng, rk[g], (0, (1 << 24) - 1, tie[g])) for g in range(8)]) for r in range(N)])
    d = complete(rng, rk, sd); z = rng.integers(0, 4, (N, 8, M)); thr = np.where(z == 0, 0, np.where(z == 1, 4096, d["thr"])); z = rng.integers(0, 4, (N, 8, M))
    ali = np.where(z == 0, 0, np.where(z == 1, M - 1, np.where(z == 2, np.arange(M), d["ali"])))
    for r in range(N):
        for g in range(8):
            q = owners(rk[g], sd[r, g])[:, ::4]; a, b = hashes(sd[r, g][:, None], ((TR + 1) * np.arange(K) + 1)[None, ::4]); e = (a * M) >> 12
            thr[q, g, e] = b; ali[q, g, e] = M - 1 - e
    d["thr"] = thr.astype(np.int32); d["ali"] = ali.astype(np.int32); return d
def setup_inputs_hot(rng):
    rk = np.stack([ranks(rng, 2800) for g in range(8)]); sd = seeds(rng, rk)
    for g in range(8):
        pool = rng.integers(0, 1 << 24, 1024); sd[rng.integers(0, N), g] = pool[rng.choice(np.flatnonzero(np.all(loads(rk[g], pool) <= CAP // 16, 1)))]
    d = complete(rng, rk, sd); h = rng.integers(0, M, (N, 8, 1)); h[:, 0] = 0; h[:, 7] = M - 1
    d["thr"] = rng.integers(0, 512, (N, 8, M)).astype(np.int32); d["ali"] = (h + np.zeros((1, 1, M), np.int64)).astype(np.int32); return d
def setup_inputs_avid(rng):
    rk = np.stack([absent(rng) for g in range(8)]); dens = rng.choice(np.array([0, 0.97, 1.0]), (N, 128)); dens[rng.integers(0, N)] = 1
    return complete(rng, rk, seeds(rng, rk), dens)
def setup_inputs_spread(rng):
    d = setup_inputs(rng); d["vec"] = wide(rng, N, 128, M); d["thr"] = (4096 >> rng.integers(0, 14, (N, 8, M))).astype(np.int32); return d
def check_inputs(d):
    bad = []
    try:
        sd, rk = d["sd"].astype(np.int64), d["rk"].astype(np.int64); w = d["seen"].astype(np.float32)
        if not ((sd >= 0) & (sd < 1 << 24)).all(): bad.append("seed")
        if not (rk == rk[:1]).all(): bad.append("rk alike on all ranks")
        if not ((rk[..., :N] >= 0) & (rk[..., :N] <= 4096) & (rk[..., N:] >= 0) & (rk[..., N:] < N)).all(): bad.append("rk")
        if not ((d["thr"] >= 0) & (d["thr"] <= 4096)).all(): bad.append("thr")
        if not ((d["ali"] >= 0) & (d["ali"] < M)).all(): bad.append("ali")
        if not ((w >= 0) & (w < 2 ** N) & (w == np.floor(w))).all(): bad.append("seen")
        if not np.isfinite(d["vec"].astype(np.float32)).all(): bad.append("finite")
        if not bad and any((np.sum(loads(rk[r, g], sd[r, 16 * g:16 * g + 16, 0]), 0) > CAP).any() for r in range(N) for g in range(8)): bad.append("cap")
    except Exception:
        bad.append("unreadable")
    return bad
def reference(sd, rk, thr, ali, seen, vec):
    chosen = np.zeros((N, 128, K), np.float32); y = np.zeros((N, 128, D), vec.dtype); n = (TR + 1) * np.arange(K); row = np.arange(16)[:, None]
    for r in range(N):
        for g in range(8):
            s = sd[r, 16 * g:16 * g + 16].astype(np.int64)
            q = owners(rk[r, g].astype(np.int64), s[:, 0])
            x = np.zeros((16, K), np.int64); done = np.zeros((16, K), bool)
            for i in range(1, TR + 1):
                a, b = hashes(s, n + i); e = (a * M) >> 12
                c = np.where(b < thr[q, g, e], e, ali[q, g, e]).astype(np.int64)
                known = (seen[q, 16 * g + row, c].astype(np.float32).astype(np.int64) >> r) & 1
                x = np.where(done, x, c); done = done | (known == 0)
            chosen[r, 16 * g:16 * g + 16] = q * M + x
            y[r, 16 * g:16 * g + 16] = vec[q.T.reshape(-1), 16 * g + row, x.T.reshape(-1)]
    return {"chosen": chosen, "y": y}

@@ -1,0 +1,592 @@
+from concourse.bass import DstId, RemoteDMATransfer
+from concourse.mybir import AluOpType as OP, ActivationFunctionType as AF
+
+M, K = 4096, 64
+H = M // 2
+MID = 1 << 24
+N1 = 1 << 23
+V_FILL = 2048
+P_FILL = [1024, 1024]
+V_LATE = 4096
+SRC = 1024
+HP = [0, 256, 1280, 2048]
+PP = [(0, 256, "psq", 0), (256, 768, "ps0", 1), (768, 1280, "ps1", 1), (1280, 1792, "ps2", 2), (1792, 2048, "ps3", 2)]
+VP = [(0, 640, 1), (640, 1408, 1), (1408, 2176, 1), (2176, 4096, 0)]
+P_ORDER = "h0 t0 t1 t2 p0 h1 w h2 p1 v1 v2 con v3".split()
+S_ORDER = "f0 f1 f2 f3 v1 v2 v3".split()
+A_ORDER = "id4 fill fill fill e0 fill e1 xs e2 ys e3 e4 fill fill fill fill fill fill".split()
+V_ORDER = ("sdf shi X0 cf Y0 X1 k0 Y1 k1 X2 k2 X4 k3 X5 k4 X6 k5 XO Y2 Y4 Y5 Y6 X7 r0 r1 vf vf am cw X8 "
+           "g0 g1 g2 g3 g4 g5 g6 Y7 Y8 vf vf vf OFF ce cmz").split()
+GT = [32, 32, 32, 48]
+HA = [64, 40, 64]
+YS = [(0, 16, "v"), (32, 48, "a"), (16, 32, "v"), (48, 64, "a")]
+PB = ["ps2", "ps3", "psq"]
+W1 = 2048
+
+SCRATCH = {
+    "fw": ("sbuf", [128, 4 * M], "bfloat16"),
+    "sr": ("sbuf", [128, M], "bfloat16"),
+    "sw": ("sbuf", [128, 4 * H], "bfloat16"),
+    "vw": ("sbuf", [128, 4 * M], "bfloat16"),
+    "fl": ("dram", [12, 128, 256], "bfloat16"),
+    "ta": ("sbuf", [128, 512], "int32"),
+    "ft": ("sbuf", [128, 768], "bfloat16"),
+    "sdi": ("sbuf", [128, 1], "int32"),
+    "shi": ("sbuf", [128, 1], "int32"),
+    "sdf": ("sbuf", [128, 1], "float32"),
+    "cf": ("sbuf", [128, 1], "float32"),
+    "rki": ("sbuf", [8, 8], "int32"),
+    "kc": ("sbuf", [8, 12], "float32"),
+    "rkf": ("sbuf", [8, 12], "float32"),
+    "f8": ("sbuf", [8, 128], "float32"),
+    "gs": ("sbuf", [8, 128], "float32"),
+    "am": ("sbuf", [128, 64], "int32"),
+    "cw": ("sbuf", [128, 64], "float32"),
+    "og": ("sbuf", [128, 448], "bfloat16"),
+    "idt": ("sbuf", [128, 128], "bfloat16"),
+    "id4k": ("sbuf", [128, 128], "bfloat16"),
+    "id16": ("sbuf", [128, 128], "bfloat16"),
+    "cm": ("sbuf", [128, 2208], "bfloat16"),
+    "n1": ("sbuf", [128, 320], "int32"),
+    "hx": ("sbuf", [128, 320], "int32"),
+    "hl": ("sbuf", [128, 320], "int32"),
+    "hs": ("sbuf", [128, 320], "float32"),
+    "hs2": ("sbuf", [128, 320], "int32"),
+    "hb": ("sbuf", [128, 320], "int32"),
+    "cb": ("sbuf", [128, 320], "float32"),
+    "ht2": ("sbuf", [128, 320], "int32"),
+    "ha": ("sbuf", [128, 320], "int32"),
+    "ce": ("sbuf", [128, 256], "float32"),
+    "off": ("sbuf", [128, 256], "float32"),
+    "l1": ("sbuf", [128, 256], "uint16"),
+    "l2": ("sbuf", [128, 192], "uint16"),
+    "l3": ("sbuf", [128, 64], "uint16"),
+    "xi": ("sbuf", [128, 256], "int32"),
+    "ah": ("sbuf", [128, 192], "int32"),
+    "ai": ("sbuf", [128, 256], "int32"),
+    "mh": ("sbuf", [128, 192], "float32"),
+    "cc": ("sbuf", [128, 256], "float32"),
+    "vi": ("sbuf", [128, 192], "int32"),
+    "vb": ("sbuf", [128, 192], "int32"),
+    "uu": ("sbuf", [128, 192], "float32"),
+    "xx": ("sbuf", [128, 64], "float32"),
+    "yt": ("sbuf", [128, 1024], "bfloat16"),
+    "on": ("sbuf", [128, 128], "bfloat16"),
+    "o16": ("sbuf", [128, 128], "bfloat16"),
+    "psr": ("psum", [128, 512], "float32"),
+    "psv": ("psum", [128, 512], "float32"),
+    "psq": ("psum", [128, 512], "float32"),
+    "psk": ("psum", [128, 512], "float32"),
+}
+for _i in range(4):
+    SCRATCH["ga%d" % _i] = ("sbuf", [128, 1024], "bfloat16")
+    SCRATCH["ps%d" % _i] = ("psum", [128, 512], "float32")
+for _i in range(3):
+    SCRATCH["gb%d" % _i] = ("sbuf", [128, 1024], "bfloat16")
+
+SEMAPHORES = ["v", "a", "p", "t", "ldt", "lds", "ldr", "fx", "st", "lr", "aft0", "aft1", "aft2", "aft3", "asn", "avc"]
+SEMAPHORES += ["%s%d" % (s, j) for s in ("sn", "hs", "vc", "hv") for j in range(6)]
+
+
+def helper_of(core, T, topo):
+    free = [c for c in topo.cores_of(core) if T.rank_of(c) is None and topo.die(c) == topo.die(core)]
+    mine = [c for c in T.cores if topo.chip(c) == topo.chip(core) and topo.die(c) == topo.die(core)]
+    return free[mine.index(core)]
+
+
+def spread(g, T, topo, core, dsts, src, name, dst_ap):
+    ids = []
+    for d in dsts:
+        rid, pid, _s = topo.addr(d)
+        ids.append(DstId(rid=rid, pnc=pid))
+    mask = topo.mask(core, dsts[0])
+    for d in dsts:
+        mask &= topo.mask(core, d)
+    g.remote_dma_fused([RemoteDMATransfer(dst_ids=ids, dma_engine_mask=mask, remote_sem=T.sem[name],
+                                          srcs=[src], dsts=[dst_ap for d in dsts], alu_op=0)], local_sem=T.sem.lr)
+    return len(topo.engines(core, dsts[0]))
+
+
+def after(T, r):
+    return [T.cores[(r + k) % len(T.cores)] for k in range(1, len(T.cores))]
+
+
+def hist(b):
+    return [(b + HP[j], b + HP[j + 1]) for j in range(len(HP) - 1)]
+
+
+def pieces(b):
+    return [(b + x0, b + x1, by) for x0, x1, by in VP]
+
+
+def helper_program(g, core, T, topo, owner):
+    r = T.rank_of(owner)
+    ne = len(topo.engines(owner, core))
+    dsts = after(T, r)
+    hp, vp = hist(H * r), pieces(M * r)
+    order = [("v", 0)] + [("h", j) for j in range(len(hp))] + [("v", j) for j in range(1, len(vp)) if vp[j][2]]
+    n = 0
+    for c, j in order:
+        x0, x1 = (hp if c == "h" else vp)[j][:2]
+        win, arr, name = (T.sw, "hs%d" % j, "asn") if c == "h" else (T.vw, "hv%d" % j, "avc")
+        g.wait_ge(T.sem[arr], ne)
+        n += spread(g, T, topo, core, dsts, win[:, x0:x1], name, win[:, x0:x1])
+    g.wait_ge(T.sem.lr, n)
+
+
+def rank_program(g, core, T, topo):
+    rank = T.rank_of(core)
+    if rank is None:
+        for c in T.cores:
+            if c in topo.cores_of(core) and helper_of(c, T, topo) == core:
+                helper_program(g, core, T, topo, c)
+        return
+
+    others = after(T, rank)
+    hc = helper_of(core, T, topo)
+    ne = len(topo.engines(core, hc))
+    b0 = M * rank
+    hp, vp = hist(H * rank), pieces(b0)
+    engs = {"v": g.vector, "a": g.scalar, "p": g, "t": g.tensor, "s": g.sync}
+    cnt = {}
+    seen = {k: {} for k in engs}
+    tok = {}
+
+    def need(q, toks):
+        for name, val in toks:
+            if seen[q].get(name, 0) < val:
+                engs[q].wait_ge(T.sem[name], val)
+                seen[q][name] = val
+
+    def done(q, ins, n=1, sem=None):
+        s = sem or q
+        ins.then_inc(T.sem[s], n)
+        cnt[s] = cnt.get(s, 0) + n
+        return (s, cnt[s])
+
+    v, a, t = g.vector, g.scalar, g.tensor
+
+    def TT(out, x, y, op, *deps):
+        need("v", deps)
+        return done("v", v.tensor_tensor(out, x, y, op))
+
+    def TS(out, x, s1, op0, s2, op1, *deps):
+        need("v", deps)
+        if op1 is None:
+            return done("v", v.tensor_scalar(out, x, s1, None, op0))
+        return done("v", v.tensor_scalar(out, x, s1, s2, op0, op1))
+
+    def CP(out, x, *deps):
+        need("v", deps)
+        return done("v", v.tensor_copy(out, x))
+
+    def FILL(ap, c):
+        return done("v", v.memset(ap, c))
+
+    def COPY(out, x, scale, *deps):
+        need("a", deps)
+        return done("a", a.activation(out, x, AF.Copy, scale=scale))
+
+    def SQUARE(out, x, scale, bias, *deps):
+        need("a", deps)
+        return done("a", a.activation(out, x, AF.Square, bias=bias, scale=scale))
+
+    def SEL(out, x, pattern, op, base, ch, *deps):
+        need("p", deps)
+        return done("p", g.affine_select(out, x, pattern, op, 0.0, base, ch))
+
+    def CONST(out, pattern, c):
+        return done("p", g.iota(out, pattern, c, 0, allow_small_or_imprecise_dtypes=True))
+
+    def dma(q, out, x, sem, *deps):
+        need(q, deps)
+        return done(q, engs[q].dma_start(out, x), 16, sem)
+
+    def send(dsts, win, x0, x1, sem):
+        return spread(g, T, topo, core, dsts, win[:, x0:x1], sem, win[:, x0:x1])
+
+    ld_v = [None] * len(VP)
+
+    def s_vec(j):
+        x0, x1, by = vp[j]
+        ld_v[j] = dma("s", T.vw[:, x0:x1], T.vec[:, x0 - b0:x1 - b0], "vc%d" % j)
+
+    def ld_seen(j):
+        return dma("s", T.sr[:, 2 * HP[j]:2 * HP[j + 1]], T.seen[:, 2 * HP[j]:2 * HP[j + 1]], "sn%d" % j)
+
+    ld_s = dma("a", T.sdi[:, :], T.sd[:, :], "lds")
+    s_vec(0)
+    dma("s", T.ta[:, 256:512], T.ali[:, :], "ldt")
+    ld_t = dma("a", T.ta[:, 0:256], T.thr[:, :], "ldt")
+    ld_r = dma("s", T.rki[:, :], T.rk[:, :], "ldr")
+    ld_sn = [ld_seen(j) for j in range(len(HP) - 1)]
+
+    regions = []
+
+    def col(x):
+        return (b0 + x) % (4 * M)
+
+    def blocks(x0, x1):
+        out = []
+        while x0 < x1:
+            e = min(x1, (x0 // M + 1) * M)
+            out.append((x0, e, col(x0)))
+            x0 = e
+        return out
+
+    cs = col(4 * M - SRC)
+    t_on = FILL(T.on[:, :], 1.0)
+    t_o16 = FILL(T.o16[:, :], 16.0)
+    t_src = FILL(T.fw[:, cs:cs + SRC], 1.0)
+    regions.append((4 * M - SRC, 4 * M, t_src))
+    t_f8 = FILL(T.f8[:, :], 1.0)
+    for x0, x1, c in blocks(0, V_FILL):
+        regions.append((x0, x1, FILL(T.fw[:, c:c + x1 - x0], 1.0)))
+    t_w0 = FILL(T.cm[:, W1:W1 + 144], 0.0)
+
+    t_n1 = done("p", g.iota(T.n1[:, :], [[1597, 5], [5 * 1597, 64]], -N1, 0))
+    t_id = SEL(T.idt[:, :], T.on[:, :], [[-1, 128]], OP.is_equal, 0, 1, t_on)
+    t_id6 = SEL(T.id16[:, :], T.o16[:, :], [[-1, 128]], OP.is_equal, 0, 1, t_o16)
+    lr = [0]
+
+    def p_vec(j):
+        x0, x1, by = vp[j]
+        need("p", [ld_v[j]])
+        lr[0] += send([hc] if by else others, T.vw, x0, x1, "hv%d" % j if by else "avc")
+
+    p_vec(0)
+    CONST(T.kc[:, 0:4], [[M, 4]], 0)
+    CONST(T.kc[:, 4:8], [[-1, 4]], 0)
+    t_kc = CONST(T.kc[:, 8:11], [[1, 3]], 1)
+    t_gs = SEL(T.gs[:, :], T.f8[:, :], [[1, 128]], OP.is_ge, 0, -16, t_f8)
+    t_gs = SEL(T.gs[:, :], T.gs[:, :], [[-1, 128]], OP.is_ge, 15, 16, t_gs)
+
+    CH = {"X": (0, 192), "Y": (192, 320)}
+    sq = {"X": T.psk[:, 0:192], "Y": T.psq[:, 256:384]}
+    pk = T.psv[:, 0:256]
+    rp = T.psv[:, 256:512]
+    t_p = [None] * 3
+    q4 = T.psr[:, 64:128]
+    t_l1 = [None, None]
+    vfills = [(c0, min(c0 + 1024, x1), c + c0 - x0) for x0, x1, c in blocks(4 * M - SRC - V_LATE, 4 * M - SRC)
+              for c0 in range(x0, x1, 1024)]
+
+    def hash_step(f, s):
+        c0, c1 = CH[f]
+        c = slice(c0, c1)
+        cc = slice(max(c0, 64), c1)
+        if s == "0":
+            r = TS(T.hx[:, c], T.n1[:, c], T.sdf[:, 0:1], OP.add, 64.0, OP.mult, t_n1, tok["sdf"])
+        elif s == "1":
+            r = TS(T.hl[:, c], T.hx[:, c], 64 * 4095, OP.bitwise_and, None, None, tok[f + "0"])
+        elif s == "2":
+            r = TT(T.hs[:, c], T.hl[:, c], T.hl[:, c], OP.mult, tok[f + "1"])
+        elif s == "4":
+            r = TS(T.hs2[:, c], T.hs[:, c], 1.0 / 4096, OP.mult, T.cf[:, 0:1], OP.add, tok[f + "2"], tok["cf"])
+        elif s == "5":
+            r = TS(T.hb[:, c], T.hs2[:, c], 6, OP.arith_shift_right, 4095, OP.bitwise_and, tok[f + "4"])
+        elif s == "6":
+            r = TS(T.cb[:, cc], T.hb[:, cc], float(2 * M), OP.mult, float(M - MID), OP.add, tok[f + "5"])
+        elif s == "O":
+            r = CP(T.cb[:, 0:64], T.hb[:, 0:64], tok[f + "5"])
+        elif s == "7":
+            r = TT(T.ht2[:, c], sq[f], T.hl[:, c], OP.add, tok[f + "s"])
+        elif s == "8":
+            r = TS(T.ha[:, cc], T.ht2[:, cc], 6, OP.arith_shift_right, 4095, OP.bitwise_and, tok[f + "7"])
+        tok[f + s] = r
+
+    def vop(n):
+        if n[0] in "XY":
+            hash_step(n[0], n[1])
+        elif n == "sdf":
+            tok[n] = CP(T.sdf[:, :], T.sdi[:, :], ld_s)
+        elif n == "shi":
+            tok[n] = TS(T.shi[:, :], T.sdi[:, :], 6, OP.logical_shift_right, 64 * 4095, OP.bitwise_and, ld_s)
+        elif n == "cf":
+            tok[n] = CP(T.cf[:, :], T.shi[:, :], tok["shi"])
+        elif n == "r0":
+            tok[n] = TT(T.rkf[:, 0:8], T.rki[:, :], T.kc[:, 0:8], OP.add, ld_r, t_kc)
+        elif n == "r1":
+            tok[n] = TT(T.rkf[:, 8:11], T.kc[:, 8:11], T.rki[:, 4:7], OP.subtract, ld_r, t_kc)
+        elif n == "k0":
+            tok[n] = TS(pk, T.ta[:, 0:256], float(2 * M), OP.mult, -float(MID), OP.add, ld_t)
+        elif n == "k1":
+            tok[n] = TT(pk, pk, T.ta[:, 256:512], OP.add, tok["k0"])
+        elif n == "k2":
+            t_p[0] = CP(T.ft[:, 0:256], pk, tok["k1"])
+        elif n == "k3":
+            tok[n] = TT(rp, pk, T.ft[:, 0:256], OP.subtract, t_p[0])
+        elif n == "k4":
+            t_p[1] = CP(T.ft[:, 256:512], rp, tok["k3"])
+        elif n == "k5":
+            t_p[2] = TT(T.ft[:, 512:768], rp, T.ft[:, 256:512], OP.subtract, t_p[1])
+        elif n == "am":
+            tok[n] = TS(T.am[:, :], T.ht2[:, 0:64], 4, OP.arith_shift_right, 12288, OP.bitwise_and, tok["X7"])
+        elif n == "cw":
+            tok[n] = TT(T.cw[:, :], T.am[:, :], T.cb[:, 0:64], OP.add, tok["am"], tok["XO"])
+        elif n[0] == "g":
+            j = int(n[1])
+            lim = T.psr[:, j:j + 1] if j < 4 else float(M * (j - 3))
+            tok["og"] = TS(T.og[:, 64 * j:64 * j + 64], T.cw[:, :], lim, OP.is_ge, T.psr[:, 4 + j:5 + j], OP.mult,
+                           tok["cw"], tok["psr"])
+        elif n == "ce":
+            tok[n] = TT(T.ce[:, :], T.cb[:, 64:320], T.ha[:, 64:320], OP.add, tok["X6"], tok["Y6"], tok["X8"], tok["Y8"])
+        elif n == "OFF":
+            x = [None] * 4
+            for i in range(4):
+                x[i] = TT(T.off[:, 64 * i:64 * i + 64], T.ha[:, 64 * i + 64:64 * i + 128], q4, OP.add, tok["q4"], tok["Y8"])
+                if i >= 2:
+                    h = i - 2
+                    t_l1[h] = CP(T.l1[:, 128 * h:128 * h + 128], T.off[:, 128 * h:128 * h + 128], x[2 * h + 1])
+        elif n == "cmz":
+            tok[n] = FILL(T.cm[:, 0:W1], 0.0)
+        elif n == "vf" and vfills:
+            x0, x1, c = vfills.pop(0)
+            regions.append((x0, x1, FILL(T.fw[:, c:c + x1 - x0], 1.0)))
+
+    fills = []
+    c0 = V_FILL
+    while c0 < 4 * M - SRC - V_LATE - sum(P_FILL):
+        c1 = min(4 * M - SRC - V_LATE - sum(P_FILL), (c0 // 1024 + 1) * 1024)
+        fills.append((c0, c1))
+        c0 = c1
+    t_ev = [None] * len(PP)
+
+    def aop(n):
+        if n == "fill":
+            c0, c1 = fills.pop(0)
+            c = col(c0)
+            regions.append((c0, c1, COPY(T.fw[:, c:c + c1 - c0], T.fw[:, cs:cs + c1 - c0], 1.0, t_src)))
+        elif n == "id4":
+            tok[n] = COPY(T.id4k[:, :], T.idt[:, :], float(M), t_id)
+        elif n[0] == "e":
+            j = int(n[1])
+            x0, x1, bank, grp = PP[j]
+            ps = T[bank][:, 0:x1 - x0]
+            need("t", [ld_sn[grp], t_id, t_id6])
+            t.matmul(ps, T.idt[:, :], T.sr[:, 2 * x0:2 * x1:2], True, False)
+            x = done("t", t.matmul(ps, T.id16[:, :], T.sr[:, 2 * x0 + 1:2 * x1:2], False, True))
+            t_ev[j] = COPY(T.sw[:, H * rank + x0:H * rank + x1], ps, 1.0, x)
+        elif n == "xs":
+            SQUARE(T.psk[:, 0:64], T.cb[:, 0:64], 1.0, 0.0, tok["XO"])
+            tok["Xs"] = SQUARE(T.psk[:, 64:192], T.cb[:, 64:192], 1.0 / (2 * M), 2047.5, tok["X6"])
+        elif n == "ys":
+            tok["Ys"] = SQUARE(sq["Y"], T.cb[:, 192:320], 1.0 / (2 * M), 2047.5, tok["Y6"])
+
+    av = list(A_ORDER)
+    ready = {"xs": ["X6", "XO"], "ys": ["Y6"]}
+
+    def a_next():
+        while av and all([x in tok for x in ready.get(av[0], [])]):
+            n = av.pop(0)
+            if n != "fill" or fills:
+                aop(n)
+
+    a_next()
+    for n in V_ORDER:
+        vop(n)
+        if n == "r1":
+            need("t", [tok["r0"], tok["r1"], t_gs])
+            tok["psr"] = done("t", t.matmul(T.psr[:, 0:11], T.gs[:, :], T.rkf[:, 0:11], True, True))
+        if n == "g6":
+            need("t", [tok["og"], tok["id4"]])
+            for j in range(7):
+                ins = t.matmul(q4, T.id4k[:, :], T.og[:, 64 * j:64 * j + 64], j == 0, j == 6)
+            tok["q4"] = done("t", ins)
+        a_next()
+    while fills:
+        aop("fill")
+    while vfills:
+        vop("vf")
+    t_ce, t_zero = tok["ce"], tok["cmz"]
+
+    def s_parts(k):
+        q = (rank + k) % 4
+        lo, hi = M * q, M * q + M
+        deps = [tk for (x0, x1, tk) in regions if x0 < M * k + M and M * k < x1]
+        deps += [t_p[2]] if k == 0 else [("aft%d" % q, 3 * len(topo.engines(T.cores[q], core)))]
+        for f in range(3):
+            x = T.ft[:, 256 * f:256 * f + 256] if k == 0 else T.fl[3 * q + f]
+            tok["fx"] = dma("s", T.fw[f::16, lo:hi], x, "fx", *deps)
+
+    wm = T.cm[:, W1 + 15:W1 + 143:16]
+
+    def p_hist(j):
+        need("p", [t_ev[i] for i in range(len(PP)) if PP[i][3] == j])
+        lr[0] += send([hc], T.sw, hp[j][0], hp[j][1], "hs%d" % j)
+
+    def p_part(f):
+        need("p", [t_p[f]])
+        lr[0] += spread(g, T, topo, core, others, T.ft[:, 256 * f:256 * f + 256], "aft%d" % rank, T.fl[3 * rank + f])
+
+    def p_fill(j):
+        y = 4 * M - SRC - V_LATE - sum(P_FILL[j:])
+        for y0, y1, c in blocks(y, y + P_FILL[j]):
+            regions.append((y0, y1, CONST(T.fw[:, c:c + y1 - y0], [[0, y1 - y0]], 1)))
+
+    def p_w(j):
+        x = SEL(wm, T.on[:, 0:8], [[-16, 8]], OP.is_ge, 0, 1, t_w0)
+        tok["w"] = SEL(wm, wm, [[16, 8]], OP.is_ge, 2, -1, x)
+
+    def p_con(j):
+        tok["con"] = SEL(T.cm[:, 0:2048:16], T.o16[:, :], [[-1, 16], [-16, 8]], OP.is_equal, 0, 1, t_zero)
+
+    calls = {"h": p_hist, "t": p_part, "v": p_vec, "p": p_fill, "w": p_w, "con": p_con, "f": s_parts}
+
+    def call(n):
+        if n in calls:
+            calls[n](0)
+        else:
+            calls[n[0]](int(n[1:]))
+
+    todo = list(S_ORDER)
+
+    def s_next():
+        n = todo.pop(0)
+        if n[0] == "v":
+            s_vec(int(n[1:]))
+        else:
+            call(n)
+
+    for n in P_ORDER:
+        while n[0] == "v" and ld_v[int(n[1:])] is None:
+            s_next()
+        call(n)
+    while todo:
+        s_next()
+
+    def diag(u):
+        return T.cm[:, W1 + 15 - u:W1 + 143 - u]
+
+    def gather(q, out, win, lst, *deps):
+        need(q, deps)
+        if q == "a":
+            return done("a", a.activation(out, win.indirect(lst), AF.Copy))
+        return done("v", v.tensor_copy(out, win.indirect(lst)))
+
+    G = [[], [], [], []]
+    E = [[], [], []]
+    d = [None] * 4
+    e = [None] * 3
+    w = [None] * 3
+    PT = [None] * 4
+    PH = [None] * 3
+    all_s = ("asn", 3 * len(hp) * ne)
+
+    def GA(q, i, c0, c1):
+        if c0 < c1:
+            G[i].append(gather(q, T["ga%d" % i][:, 16 * c0:16 * c1], T.fw[:, :], T.l1[:, 64 * i + c0:64 * i + c1],
+                               tok["fx"], t_l1[i // 2]))
+
+    def PE(i):
+        need("t", G[i] + [tok["w"]] + t_ev)
+        out = T["ps%d" % (i // 2)][:, 64 * (i % 2):64 * (i % 2) + 64]
+        for u in range(16):
+            ins = t.matmul(out, diag(u), T["ga%d" % i][:, u::16], u == 0, u == 15)
+        PT[i] = done("t", ins)
+
+    def HI(q, i, c0, c1):
+        if c0 < c1:
+            E[i].append(gather(q, T["gb%d" % i][:, 16 * c0:16 * c1], T.sw[:, :], T.l2[:, 64 * i + c0:64 * i + c1],
+                               all_s, e[i], *t_ev))
+
+    def PK(i):
+        need("t", E[i] + [tok["con"]])
+        for u in range(16):
+            ins = t.matmul(T[PB[i]][:, 256:320], T.cm[:, 127 * u:127 * u + 128], T["gb%d" % i][:, u::16], u == 0, u == 15)
+        PH[i] = done("t", ins)
+
+    def decide(j):
+        c = slice(128 * j, 128 * j + 128)
+        h = slice(128 * j, min(192, 128 * j + 128))
+        m = {}
+
+        def f0():
+            m[0] = TT(T.xi[:, c], T["ps%d" % j][:, 0:128], T.ce[:, c], OP.min, PT[2 * j + 1], t_ce)
+
+        def f1():
+            m[1] = TS(T.ai[:, c], T.xi[:, c], M - 1, OP.bitwise_and, None, None, m[0])
+
+        def f2(i):
+            ci = slice(64 * i, 64 * i + 64)
+            d[i] = TT(T.cc[:, ci], T.ai[:, ci], q4, OP.add, m[1])
+
+        def f3():
+            x = TS(T.l2[:, h], T.cc[:, h], 0.5, OP.mult, -0.25, OP.add, d[2 * j], d[2 * j + (j == 0)])
+            for i in range(2 * j, min(3, 2 * j + 2)):
+                e[i] = x
+
+        def f4():
+            m[4] = TS(T.ah[:, h], T.xi[:, h], 1, OP.bitwise_and, None, None, m[0])
+
+        def f5():
+            x = TS(T.mh[:, h], T.ah[:, h], -0.9375, OP.mult, 1.0, OP.add, m[4])
+            for i in range(2 * j, min(3, 2 * j + 2)):
+                w[i] = x
+
+        if j == 0:
+            return [f0, f1, lambda: f2(0), lambda: f2(1), f3], [f4, f5]
+        return [f0, f1, lambda: f2(2), f3], [lambda: f2(3), f4, f5]
+
+    def run(calls):
+        for f in calls:
+            f()
+
+    for i in range(4):
+        GA("a", i, 0, GT[i])
+        GA("v", i, GT[i], 64)
+        PE(i)
+    now, later = decide(0)
+    run(now)
+    HI("a", 0, 0, HA[0])
+    HI("a", 1, 0, HA[1])
+    run(later)
+    HI("v", 0, HA[0], 64)
+    PK(0)
+    now, later = decide(1)
+    run(now)
+    HI("v", 1, HA[1], 64)
+    PK(1)
+    HI("a", 2, 0, HA[2])
+    run(later)
+    HI("v", 2, HA[2], 64)
+    PK(2)
+
+    bit = 16 << rank
+
+    def has(i):
+        c = slice(64 * i, 64 * i + 64)
+        x = TT(T.vi[:, c], T[PB[i]][:, 256:320], T.mh[:, c], OP.mult, PH[i], w[i])
+        return T.vb[:, c], TS(T.vb[:, c], T.vi[:, c], bit, OP.bitwise_and, None, None, x)
+
+    x = TT(T.psv[:, 0:192], T.cc[:, 64:256], T.cc[:, 0:192], OP.subtract, *d)
+    for i in range(3):
+        x = TS(T.psv[:, 192 + 64 * i:256 + 64 * i], T.psv[:, 64 * i:64 * i + 64], float(bit) ** (-1 - i), OP.mult, None, None, x)
+    t_dc = x
+    first, keep, rest = T.psr[:, 384:448], T.psr[:, 448:512], T.psk[:, 448:512]
+    b1, b2 = T.psk[:, 320:384], T.psk[:, 384:448]
+    s1, y = has(0)
+    x = TT(T.uu[:, 0:64], s1, T.psv[:, 192:256], OP.mult, y, t_dc)
+    t_b1 = TT(b1, s1, T.psv[:, 256:320], OP.mult)
+    t_b2 = TT(b2, s1, T.psv[:, 320:384], OP.mult)
+    x = TT(first, T.uu[:, 0:64], T.cc[:, 0:64], OP.add, x)
+    s2, y = has(1)
+    z = TT(T.uu[:, 64:128], s2, b1, OP.mult, y, t_b1)
+    t_r = TT(rest, s2, b2, OP.mult, t_b2)
+    t_k = TT(keep, T.uu[:, 64:128], first, OP.add, z, x)
+    s3, y = has(2)
+    y = TT(T.uu[:, 128:192], s3, rest, OP.mult, y, t_r)
+    t_x = TT(T.xx[:, :], T.uu[:, 128:192], keep, OP.add, y, t_k)
+    t_l3 = CP(T.l3[:, :], T.xx[:, :], t_x)
+    dma("s", T.chosen[:, :], T.xx[:, :], "st", t_x)
+
+    all_v = ("avc", 3 * len(VP) * ne)
+    yq = []
+    for c0, c1, q in YS:
+        yq.append((c0, c1, gather(q, T.yt[:, 16 * c0:16 * c1], T.vw[:, :], T.l3[:, c0:c1], all_v, t_l3, *ld_v)))
+    for c0, c1, x in yq:
+        t_st = dma("s", T.y[:, 16 * c0:16 * c1], T.yt[:, 16 * c0:16 * c1], "st", x)
+
+    need("p", [("lr", lr[0])])
+    need("s", [t_st] + [(s, cnt[s]) for s in ("v", "a", "p", "t", "ldt", "lds", "ldr", "fx")])
+    need("s", ld_sn + ld_v)

@@ -4,39 +4,37 @@ from concourse.mybir import AluOpType as OP, ActivationFunctionType as AF
 M, K = 4096, 64
 H = M // 2
 MID = 1 << 24
-N1 = 1 << 23
-V_FILL = 2048
-P_FILL = [1024, 1024]
-V_LATE = 4096
+WRAP = 64 * M
+TP = ["n", "n", "s"]
+HP = [(0, 512, "n"), (512, 1536, "n"), (1536, 2048, "f")]
+VP = [(0, 128, "n"), (128, 384, "s"), (384, 640, "n"), (640, 2176, "n"), (2176, 4096, "s")]
+HELPER_ORDER = "v0 t0 t1 h0 h1 h2 v2 v3".split()
+SP = [(0, 1024), (1024, 2048)]
+PP = [(0, 512, 0), (512, 1024, 1), (1024, 1536, 1), (1536, 2048, 2)]
+LOADS = "v0 d t r s0 v1 s1".split()
 SRC = 1024
-HP = [0, 256, 1280, 2048]
-PP = [(0, 256, "psq", 0), (256, 768, "ps0", 1), (768, 1280, "ps1", 1), (1280, 1792, "ps2", 2), (1792, 2048, "ps3", 2)]
-VP = [(0, 640, 1), (640, 1408, 1), (1408, 2176, 1), (2176, 4096, 0)]
-P_ORDER = "h0 t0 t1 t2 p0 h1 w h2 p1 v1 v2 con v3".split()
-S_ORDER = "f0 f1 f2 f3 v1 v2 v3".split()
-A_ORDER = "id4 fill fill fill e0 fill e1 xs e2 ys e3 e4 fill fill fill fill fill fill".split()
-V_ORDER = ("sdf shi X0 cf Y0 X1 k0 Y1 k1 X2 k2 X4 k3 X5 k4 X6 k5 XO Y2 Y4 Y5 Y6 X7 r0 r1 vf vf am cw X8 "
-           "g0 g1 g2 g3 g4 g5 g6 Y7 Y8 vf vf vf OFF ce cmz").split()
-GT = [32, 32, 32, 48]
-HA = [64, 40, 64]
-YS = [(0, 16, "v"), (32, 48, "a"), (16, 32, "v"), (48, 64, "a")]
-PB = ["ps2", "ps3", "psq"]
-W1 = 2048
+P_ORDER = "kc v0 Z:1024 v1 t0 gs t1 t2 h0 F:512 h1 h2 wt v2 v3 con v4".split()
+S_ORDER = "f0 f1 f2 f3 v2 v3 v4 chosen y:0:16 y:32:48 y:16:32 y:48:64".split()
+A_ORDER = ("F:1024 id16 F:256 Xc F:512 Yc F:256 X2 F:512 Y2 F:512 e0 id4 F:512 Xs e1 F:512 e2 Ys e3 F:768 F:512 "
+           "T0:0:30 T1:0:32 T2:0:40 T3:0:64 H0:0:40 H1:0:40 H2:0:34 V0:32:48 V0:48:64").split()
+V_ORDER = ("lo hi l64 F:256 th cf F:256 X0 Y0 X1 k0 F:256 Y1 k1 X4 k2 X5 k3 XO r0 F:256 X6 Y4 k4 F:768 k5 r1 Y5 X7 F:512 "
+           "am Y6 cw X8 g0 g1 g2 g3 g4 g5 g6 F:768 F:768 F:256 Y7 F:256 Y8 F:1024 o0 o1 o2 o3 Xl Yl Z:1024 ceX ceY "
+           "T0:30:64 T1:32:64 T2:40:64 m0 a0 b0 c0 w0 m1 i0 a1 b1 H0:40:48 w1 c1 H0:48:64 i1 m2 d0 a2 b2 H1:40:52 c2 w2 "
+           "H1:52:64 i2 d1 m3 H2:34:44 n0 a3 H2:44:64 s0 d2 u0 n1 first s1 w01 u1 rest keep n2 s2 u2 x l3 V0:0:16 V0:16:32").split()
+T_ORDER = "p0 p1 p2 p3 psr q4 T0 T1 T2 T3 H0 H1 H2".split()
 
 SCRATCH = {
     "fw": ("sbuf", [128, 4 * M], "bfloat16"),
-    "sr": ("sbuf", [128, M], "bfloat16"),
     "sw": ("sbuf", [128, 4 * H], "bfloat16"),
     "vw": ("sbuf", [128, 4 * M], "bfloat16"),
     "fl": ("dram", [12, 128, 256], "bfloat16"),
     "ta": ("sbuf", [128, 512], "int32"),
     "ft": ("sbuf", [128, 768], "bfloat16"),
     "sdi": ("sbuf", [128, 1], "int32"),
-    "shi": ("sbuf", [128, 1], "int32"),
-    "sdf": ("sbuf", [128, 1], "float32"),
-    "cf": ("sbuf", [128, 1], "float32"),
+    "col": ("sbuf", [128, 2], "int32"),
+    "cf": ("sbuf", [128, 4], "float32"),
     "rki": ("sbuf", [8, 8], "int32"),
-    "kc": ("sbuf", [8, 12], "float32"),
+    "kc": ("sbuf", [8, 8], "float32"),
     "rkf": ("sbuf", [8, 12], "float32"),
     "f8": ("sbuf", [8, 128], "float32"),
     "gs": ("sbuf", [8, 128], "float32"),
@@ -46,14 +44,16 @@ SCRATCH = {
     "idt": ("sbuf", [128, 128], "bfloat16"),
     "id4k": ("sbuf", [128, 128], "bfloat16"),
     "id16": ("sbuf", [128, 128], "bfloat16"),
-    "cm": ("sbuf", [128, 2208], "bfloat16"),
+    "cm": ("sbuf", [128, 2048], "bfloat16"),
+    "c0": ("sbuf", [128, 144], "bfloat16"),
     "n1": ("sbuf", [128, 320], "int32"),
-    "hx": ("sbuf", [128, 320], "int32"),
-    "hl": ("sbuf", [128, 320], "int32"),
+    "n2": ("sbuf", [128, 320], "int32"),
+    "c64": ("sbuf", [128, 320], "float32"),
+    "hx": ("sbuf", [128, 320], "float32"),
     "hs": ("sbuf", [128, 320], "float32"),
     "hs2": ("sbuf", [128, 320], "int32"),
     "hb": ("sbuf", [128, 320], "int32"),
-    "cb": ("sbuf", [128, 320], "float32"),
+    "sq": ("sbuf", [128, 320], "float32"),
     "ht2": ("sbuf", [128, 320], "int32"),
     "ha": ("sbuf", [128, 320], "int32"),
     "ce": ("sbuf", [128, 256], "float32"),
@@ -65,18 +65,17 @@ SCRATCH = {
     "ah": ("sbuf", [128, 192], "int32"),
     "ai": ("sbuf", [128, 256], "int32"),
     "mh": ("sbuf", [128, 192], "float32"),
-    "cc": ("sbuf", [128, 256], "float32"),
+    "cc": ("sbuf", [128, 192], "float32"),
     "vi": ("sbuf", [128, 192], "int32"),
     "vb": ("sbuf", [128, 192], "int32"),
-    "uu": ("sbuf", [128, 192], "float32"),
+    "uu": ("sbuf", [128, 256], "float32"),
     "xx": ("sbuf", [128, 64], "float32"),
     "yt": ("sbuf", [128, 1024], "bfloat16"),
     "on": ("sbuf", [128, 128], "bfloat16"),
-    "o16": ("sbuf", [128, 128], "bfloat16"),
     "psr": ("psum", [128, 512], "float32"),
     "psv": ("psum", [128, 512], "float32"),
-    "psq": ("psum", [128, 512], "float32"),
-    "psk": ("psum", [128, 512], "float32"),
+    "psx": ("psum", [128, 512], "float32"),
+    "psy": ("psum", [128, 512], "float32"),
 }
 for _i in range(4):
     SCRATCH["ga%d" % _i] = ("sbuf", [128, 1024], "bfloat16")
@@ -84,8 +83,8 @@ for _i in range(4):
 for _i in range(3):
     SCRATCH["gb%d" % _i] = ("sbuf", [128, 1024], "bfloat16")
 
-SEMAPHORES = ["v", "a", "p", "t", "ldt", "lds", "ldr", "fx", "st", "lr", "aft0", "aft1", "aft2", "aft3", "asn", "avc"]
-SEMAPHORES += ["%s%d" % (s, j) for s in ("sn", "hs", "vc", "hv") for j in range(6)]
+SEMAPHORES = ["v", "a", "p", "t", "ldt", "lds", "ldr", "fx", "st", "lr", "aft0", "aft1", "aft2", "aft3", "ah", "av"]
+SEMAPHORES += ["%s%d" % (s, j) for s in ("sn", "t", "h", "vc", "v") for j in range(6)]
 
 
 def helper_of(core, T, topo):
@@ -111,26 +110,31 @@ def after(T, r):
     return [T.cores[(r + k) % len(T.cores)] for k in range(1, len(T.cores))]
 
 
-def hist(b):
-    return [(b + HP[j], b + HP[j + 1]) for j in range(len(HP) - 1)]
+def across(core, T, topo):
+    mine = [c for c in T.cores if topo.die(c) == topo.die(core)]
+    return [c for c in T.cores if c not in mine][mine.index(core)]
 
 
-def pieces(b):
-    return [(b + x0, b + x1, by) for x0, x1, by in VP]
+def piece(T, r, n):
+    if n[0] == "t":
+        return T.fl[3 * r + int(n[1])], "aft%d" % r, TP[int(n[1])]
+    x0, x1, way = (HP if n[0] == "h" else VP)[int(n[1])]
+    b = (H if n[0] == "h" else M) * r
+    return (T.sw if n[0] == "h" else T.vw)[:, b + x0:b + x1], "a" + n[0], way
 
 
-def helper_program(g, core, T, topo, owner):
-    r = T.rank_of(owner)
-    ne = len(topo.engines(owner, core))
-    dsts = after(T, r)
-    hp, vp = hist(H * r), pieces(M * r)
-    order = [("v", 0)] + [("h", j) for j in range(len(hp))] + [("v", j) for j in range(1, len(vp)) if vp[j][2]]
+def helper_program(g, core, T, topo, near):
+    far = across(near, T, topo)
     n = 0
-    for c, j in order:
-        x0, x1 = (hp if c == "h" else vp)[j][:2]
-        win, arr, name = (T.sw, "hs%d" % j, "asn") if c == "h" else (T.vw, "hv%d" % j, "avc")
-        g.wait_ge(T.sem[arr], ne)
-        n += spread(g, T, topo, core, dsts, win[:, x0:x1], name, win[:, x0:x1])
+    for name in HELPER_ORDER:
+        way = piece(T, 0, name)[2]
+        if way == "n":
+            owner, dsts = near, after(T, T.rank_of(near))
+        else:
+            owner, dsts = far, [c for c in after(T, T.rank_of(far)) if topo.die(c) == topo.die(core)]
+        x, sem, way = piece(T, T.rank_of(owner), name)
+        g.wait_ge(T.sem[name], len(topo.engines(owner, core)))
+        n += spread(g, T, topo, core, dsts, x, sem, x)
     g.wait_ge(T.sem.lr, n)
 
 
@@ -146,7 +150,6 @@ def rank_program(g, core, T, topo):
     hc = helper_of(core, T, topo)
     ne = len(topo.engines(core, hc))
     b0 = M * rank
-    hp, vp = hist(H * rank), pieces(b0)
     engs = {"v": g.vector, "a": g.scalar, "p": g, "t": g.tensor, "s": g.sync}
     cnt = {}
     seen = {k: {} for k in engs}
@@ -163,6 +166,9 @@ def rank_program(g, core, T, topo):
         ins.then_inc(T.sem[s], n)
         cnt[s] = cnt.get(s, 0) + n
         return (s, cnt[s])
+
+    def toks(*names):
+        return [tok[n] for n in names]
 
     v, a, t = g.vector, g.scalar, g.tensor
 
@@ -187,9 +193,9 @@ def rank_program(g, core, T, topo):
         need("a", deps)
         return done("a", a.activation(out, x, AF.Copy, scale=scale))
 
-    def SQUARE(out, x, scale, bias, *deps):
+    def ACT(out, x, func, scale, bias, *deps):
         need("a", deps)
-        return done("a", a.activation(out, x, AF.Square, bias=bias, scale=scale))
+        return done("a", a.activation(out, x, func, bias=bias, scale=scale))
 
     def SEL(out, x, pattern, op, base, ch, *deps):
         need("p", deps)
@@ -202,391 +208,333 @@ def rank_program(g, core, T, topo):
         need(q, deps)
         return done(q, engs[q].dma_start(out, x), 16, sem)
 
-    def send(dsts, win, x0, x1, sem):
-        return spread(g, T, topo, core, dsts, win[:, x0:x1], sem, win[:, x0:x1])
-
-    ld_v = [None] * len(VP)
+    def group(out, pairs, *deps):
+        need("t", deps)
+        for j, (w, x) in enumerate(pairs):
+            ins = t.matmul(out, w, x, j == 0, j == len(pairs) - 1)
+        return ins
 
     def s_vec(j):
-        x0, x1, by = vp[j]
-        ld_v[j] = dma("s", T.vw[:, x0:x1], T.vec[:, x0 - b0:x1 - b0], "vc%d" % j)
+        x0, x1, way = VP[j]
+        tok["lv%d" % j] = dma("s", T.vw[:, b0 + x0:b0 + x1], T.vec[:, x0:x1], "vc%d" % j)
 
-    def ld_seen(j):
-        return dma("s", T.sr[:, 2 * HP[j]:2 * HP[j + 1]], T.seen[:, 2 * HP[j]:2 * HP[j + 1]], "sn%d" % j)
+    def s_seen(j):
+        x0, x1 = SP[j]
+        tok["ls%d" % j] = dma("s", T.fw[:, b0 + 2 * x0:b0 + 2 * x1], T.seen[:, 2 * x0:2 * x1], "sn%d" % j)
 
-    ld_s = dma("a", T.sdi[:, :], T.sd[:, :], "lds")
-    s_vec(0)
-    dma("s", T.ta[:, 256:512], T.ali[:, :], "ldt")
-    ld_t = dma("a", T.ta[:, 0:256], T.thr[:, :], "ldt")
-    ld_r = dma("s", T.rki[:, :], T.rk[:, :], "ldr")
-    ld_sn = [ld_seen(j) for j in range(len(HP) - 1)]
+    for n in LOADS:
+        if n[0] == "v":
+            s_vec(int(n[1]))
+        elif n == "d":
+            ld_s = dma("a", T.sdi[:, :], T.sd[:, :], "lds")
+        elif n == "t":
+            dma("s", T.ta[:, 256:512], T.ali[:, :], "ldt")
+            ld_t = dma("a", T.ta[:, 0:256], T.thr[:, :], "ldt")
+        elif n == "r":
+            ld_r = dma("s", T.rki[:, :], T.rk[:, :], "ldr")
+        else:
+            s_seen(int(n[1]))
 
-    regions = []
+    filled = []
+    upto = [M]
 
-    def col(x):
-        return (b0 + x) % (4 * M)
+    def fill(q, w):
+        x0 = upto[0]
+        x1 = min(x0 + w, (x0 // M + 1) * M)
+        upto[0] = x1
+        c = (b0 + x0) % (4 * M)
+        out = T.fw[:, c:c + x1 - x0]
+        if q == "v":
+            r = FILL(out, 1.0)
+        elif q == "a":
+            r = COPY(out, T.fw[:, cs:cs + x1 - x0], 1.0, t_src)
+        else:
+            r = CONST(out, [[0, x1 - x0]], 1)
+        filled.append(r)
+        if x1 % M == 0 or x1 == 4 * M - SRC:
+            tok["full%d" % (x0 // M)] = list(filled)
+        return fill(q, w - (x1 - x0)) if x1 - x0 < w else r
 
-    def blocks(x0, x1):
-        out = []
-        while x0 < x1:
-            e = min(x1, (x0 // M + 1) * M)
-            out.append((x0, e, col(x0)))
-            x0 = e
-        return out
+    zeros = []
 
-    cs = col(4 * M - SRC)
+    def zero(q, w):
+        x0 = sum([n for n, r in zeros])
+        out = T.cm[:, x0:x0 + w]
+        if q == "v":
+            r = FILL(out, 0.0)
+        elif q == "a":
+            r = COPY(out, T.sw[:, H * rank:H * rank + w], 0.0, *toks(*moved))
+        else:
+            r = CONST(out, [[0, w]], 0)
+        zeros.append((w, r))
+        if x0 + w == H:
+            tok["zeros"] = [r for n, r in zeros]
+        return r
+
+    t_n1 = done("p", g.iota(T.n1[:, :], [[1597, 5], [5 * 1597, 64]], 0, 0))
+    cs = (b0 - SRC) % (4 * M)
     t_on = FILL(T.on[:, :], 1.0)
-    t_o16 = FILL(T.o16[:, :], 16.0)
     t_src = FILL(T.fw[:, cs:cs + SRC], 1.0)
-    regions.append((4 * M - SRC, 4 * M, t_src))
+    filled.append(t_src)
     t_f8 = FILL(T.f8[:, :], 1.0)
-    for x0, x1, c in blocks(0, V_FILL):
-        regions.append((x0, x1, FILL(T.fw[:, c:c + x1 - x0], 1.0)))
-    t_w0 = FILL(T.cm[:, W1:W1 + 144], 0.0)
-
-    t_n1 = done("p", g.iota(T.n1[:, :], [[1597, 5], [5 * 1597, 64]], -N1, 0))
     t_id = SEL(T.idt[:, :], T.on[:, :], [[-1, 128]], OP.is_equal, 0, 1, t_on)
-    t_id6 = SEL(T.id16[:, :], T.o16[:, :], [[-1, 128]], OP.is_equal, 0, 1, t_o16)
-    lr = [0]
-
-    def p_vec(j):
-        x0, x1, by = vp[j]
-        need("p", [ld_v[j]])
-        lr[0] += send([hc] if by else others, T.vw, x0, x1, "hv%d" % j if by else "avc")
-
-    p_vec(0)
-    CONST(T.kc[:, 0:4], [[M, 4]], 0)
-    CONST(T.kc[:, 4:8], [[-1, 4]], 0)
-    t_kc = CONST(T.kc[:, 8:11], [[1, 3]], 1)
-    t_gs = SEL(T.gs[:, :], T.f8[:, :], [[1, 128]], OP.is_ge, 0, -16, t_f8)
-    t_gs = SEL(T.gs[:, :], T.gs[:, :], [[-1, 128]], OP.is_ge, 15, 16, t_gs)
+    x = TS(T.n2[:, :], T.n1[:, :], M - 1, OP.bitwise_and, None, None, t_n1)
+    t_w0 = FILL(T.c0[:, :], 0.0)
+    t_c64 = TS(T.c64[:, :], T.n2[:, :], 64.0, OP.mult, None, None, x)
 
     CH = {"X": (0, 192), "Y": (192, 320)}
-    sq = {"X": T.psk[:, 0:192], "Y": T.psq[:, 256:384]}
-    pk = T.psv[:, 0:256]
-    rp = T.psv[:, 256:512]
-    t_p = [None] * 3
+    hl = {"X": T.psx[:, 0:192], "Y": T.psy[:, 0:128]}
+    raw = {"X": T.psx[:, 192:384], "Y": T.psy[:, 128:256]}
+    cb = {"X": T.psx[:, 384:512], "Y": T.psy[:, 256:384]}
+    ob = T.psx[:, 192:256]
+    l64, th, cf = [T.cf[:, j:j + 1] for j in range(3)]
+    pk, rp = T.psv[:, 0:256], T.psv[:, 256:512]
     q4 = T.psr[:, 64:128]
-    t_l1 = [None, None]
-    vfills = [(c0, min(c0 + 1024, x1), c + c0 - x0) for x0, x1, c in blocks(4 * M - SRC - V_LATE, 4 * M - SRC)
-              for c0 in range(x0, x1, 1024)]
+    packed = ["p%d" % j for j in range(len(PP))]
+    moved = ["e%d" % j for j in range(len(PP))]
 
     def hash_step(f, s):
         c0, c1 = CH[f]
         c = slice(c0, c1)
         cc = slice(max(c0, 64), c1)
+        if s == "c":
+            return ACT(raw[f], T.c64[:, c], AF.Identity, 1.0, l64, t_c64, tok["l64"])
         if s == "0":
-            r = TS(T.hx[:, c], T.n1[:, c], T.sdf[:, 0:1], OP.add, 64.0, OP.mult, t_n1, tok["sdf"])
-        elif s == "1":
-            r = TS(T.hl[:, c], T.hx[:, c], 64 * 4095, OP.bitwise_and, None, None, tok[f + "0"])
-        elif s == "2":
-            r = TT(T.hs[:, c], T.hl[:, c], T.hl[:, c], OP.mult, tok[f + "1"])
-        elif s == "4":
-            r = TS(T.hs2[:, c], T.hs[:, c], 1.0 / 4096, OP.mult, T.cf[:, 0:1], OP.add, tok[f + "2"], tok["cf"])
-        elif s == "5":
-            r = TS(T.hb[:, c], T.hs2[:, c], 6, OP.arith_shift_right, 4095, OP.bitwise_and, tok[f + "4"])
-        elif s == "6":
-            r = TS(T.cb[:, cc], T.hb[:, cc], float(2 * M), OP.mult, float(M - MID), OP.add, tok[f + "5"])
-        elif s == "O":
-            r = CP(T.cb[:, 0:64], T.hb[:, 0:64], tok[f + "5"])
-        elif s == "7":
-            r = TT(T.ht2[:, c], sq[f], T.hl[:, c], OP.add, tok[f + "s"])
-        elif s == "8":
-            r = TS(T.ha[:, cc], T.ht2[:, cc], 6, OP.arith_shift_right, 4095, OP.bitwise_and, tok[f + "7"])
-        tok[f + s] = r
+            return TS(T.hx[:, c], T.c64[:, c], th, OP.is_ge, -float(WRAP), OP.mult, t_c64, tok["th"])
+        if s == "1":
+            return TT(hl[f], raw[f], T.hx[:, c], OP.add, tok[f + "0"], tok[f + "c"])
+        if s == "2":
+            return ACT(T.hs[:, c], hl[f], AF.Square, 1.0 / 64, 0.0, tok[f + "1"])
+        if s == "4":
+            return TS(T.hs2[:, c], T.hs[:, c], cf, OP.add, None, None, tok[f + "2"], tok["cf"])
+        if s == "5":
+            return TS(T.hb[:, c], T.hs2[:, c], 6, OP.arith_shift_right, 4095, OP.bitwise_and, tok[f + "4"])
+        if s == "6":
+            return TS(cb[f], T.hb[:, cc], float(2 * M), OP.mult, float(M - MID), OP.add, tok[f + "5"])
+        if s == "O":
+            return CP(ob, T.hb[:, 0:64], tok[f + "5"])
+        if s == "s":
+            x = tok[f + "6"]
+            if f == "X":
+                ACT(T.sq[:, 0:64], ob, AF.Square, 1.0, 0.0, tok["XO"], x)
+            return ACT(T.sq[:, cc], cb[f], AF.Square, 1.0 / (2 * M), 2047.5, x)
+        if s == "7":
+            return TT(T.ht2[:, c], hl[f], T.sq[:, c], OP.add, tok[f + "s"])
+        if s == "8":
+            return TS(T.ha[:, cc], T.ht2[:, cc], 6, OP.arith_shift_right, 4095, OP.bitwise_and, tok[f + "7"])
+        i = (cc.start - 64) // 64
+        return CP(T.l1[:, c1 - 192:c1 - 64], T.off[:, c1 - 192:c1 - 64], *toks("o%d" % i, "o%d" % (i + 1)))
+
+    parts = {}
+    all_s = ("ah", 3 * len(HP) * ne)
+    all_v = ("av", 3 * len(VP) * ne)
+
+    def look(q, n):
+        if n[0] in "FZ":
+            return (fill if n[0] == "F" else zero)(q, int(n[2:]))
+        name, c0, c1 = n.split(":")
+        i, c0, c1 = int(name[1]), int(c0), int(c1)
+        out, win, lst, deps = {
+            "T": lambda: (T["ga%d" % i], T.fw, T.l1, [max(toks("f0", "f1", "f2", "f3")), tok["XY"[i // 2] + "l"]]),
+            "H": lambda: (T["gb%d" % i], T.sw, T.l2, [all_s] + toks("i%d" % i, *moved)),
+            "V": lambda: (T.yt, T.vw, T.l3, [all_v] + toks("l3", *["lv%d" % j for j in range(len(VP))]))}[name[0]]()
+        out, x = out[:, 16 * c0:16 * c1], win[:, :].indirect(lst[:, 64 * i + c0:64 * i + c1])
+        r = CP(out, x, *deps) if q == "v" else COPY(out, x, 1.0, *deps)
+        parts[name] = parts.get(name, []) + [(c1 - c0, r)]
+        if sum([w for w, r in parts[name]]) == K:
+            tok["g" + name] = [r for w, r in parts[name]]
+        return r
+
+    first, keep, rest = T.psv[:, 192:256], T.psv[:, 256:320], T.psv[:, 320:384]
 
     def vop(n):
+        j = int(n[1:]) if n[1:].isdigit() else 0
+        c = slice(64 * j, 64 * j + 64)
+        if ":" in n:
+            return look("v", n)
         if n[0] in "XY":
-            hash_step(n[0], n[1])
-        elif n == "sdf":
-            tok[n] = CP(T.sdf[:, :], T.sdi[:, :], ld_s)
-        elif n == "shi":
-            tok[n] = TS(T.shi[:, :], T.sdi[:, :], 6, OP.logical_shift_right, 64 * 4095, OP.bitwise_and, ld_s)
-        elif n == "cf":
-            tok[n] = CP(T.cf[:, :], T.shi[:, :], tok["shi"])
-        elif n == "r0":
-            tok[n] = TT(T.rkf[:, 0:8], T.rki[:, :], T.kc[:, 0:8], OP.add, ld_r, t_kc)
-        elif n == "r1":
-            tok[n] = TT(T.rkf[:, 8:11], T.kc[:, 8:11], T.rki[:, 4:7], OP.subtract, ld_r, t_kc)
-        elif n == "k0":
-            tok[n] = TS(pk, T.ta[:, 0:256], float(2 * M), OP.mult, -float(MID), OP.add, ld_t)
-        elif n == "k1":
-            tok[n] = TT(pk, pk, T.ta[:, 256:512], OP.add, tok["k0"])
-        elif n == "k2":
-            t_p[0] = CP(T.ft[:, 0:256], pk, tok["k1"])
-        elif n == "k3":
-            tok[n] = TT(rp, pk, T.ft[:, 0:256], OP.subtract, t_p[0])
-        elif n == "k4":
-            t_p[1] = CP(T.ft[:, 256:512], rp, tok["k3"])
-        elif n == "k5":
-            t_p[2] = TT(T.ft[:, 512:768], rp, T.ft[:, 256:512], OP.subtract, t_p[1])
-        elif n == "am":
-            tok[n] = TS(T.am[:, :], T.ht2[:, 0:64], 4, OP.arith_shift_right, 12288, OP.bitwise_and, tok["X7"])
-        elif n == "cw":
-            tok[n] = TT(T.cw[:, :], T.am[:, :], T.cb[:, 0:64], OP.add, tok["am"], tok["XO"])
-        elif n[0] == "g":
-            j = int(n[1])
+            return hash_step(n[0], n[1])
+        if n == "lo":
+            return TS(T.col[:, 0:1], T.sdi[:, :], M - 1, OP.bitwise_and, None, None, ld_s)
+        if n == "l64":
+            return TS(l64, T.col[:, 0:1], 64.0, OP.mult, None, None, tok["lo"])
+        if n == "th":
+            return TS(th, T.col[:, 0:1], -64.0, OP.mult, float(WRAP), OP.add, tok["lo"])
+        if n == "hi":
+            return TS(T.col[:, 1:2], T.sdi[:, :], 6, OP.logical_shift_right, 64 * 4095, OP.bitwise_and, ld_s)
+        if n == "cf":
+            return CP(cf, T.col[:, 1:2], tok["hi"])
+        if n == "r0":
+            return TT(T.rkf[:, 0:8], T.rki[:, :], T.kc[:, 0:8], OP.add, ld_r, tok["kc"])
+        if n == "r1":
+            return TS(T.rkf[:, 8:11], T.rkf[:, 4:7], -1.0, OP.mult, 1.0, OP.add, tok["r0"])
+        if n == "k0":
+            return TS(pk, T.ta[:, 0:256], float(2 * M), OP.mult, -float(MID), OP.add, ld_t)
+        if n == "k1":
+            return TT(pk, pk, T.ta[:, 256:512], OP.add, tok["k0"])
+        if n == "k2":
+            return CP(T.ft[:, 0:256], pk, tok["k1"])
+        if n == "k3":
+            return TT(rp, pk, T.ft[:, 0:256], OP.subtract, tok["k2"])
+        if n == "k4":
+            return CP(T.ft[:, 256:512], rp, tok["k3"])
+        if n == "k5":
+            return TT(T.ft[:, 512:768], rp, T.ft[:, 256:512], OP.subtract, tok["k4"])
+        if n == "am":
+            return TS(T.am[:, :], T.ht2[:, 0:64], 4, OP.arith_shift_right, 12288, OP.bitwise_and, tok["X7"])
+        if n == "cw":
+            return TT(T.cw[:, :], ob, T.am[:, :], OP.add, tok["am"])
+        if n[0] == "g":
             lim = T.psr[:, j:j + 1] if j < 4 else float(M * (j - 3))
-            tok["og"] = TS(T.og[:, 64 * j:64 * j + 64], T.cw[:, :], lim, OP.is_ge, T.psr[:, 4 + j:5 + j], OP.mult,
-                           tok["cw"], tok["psr"])
-        elif n == "ce":
-            tok[n] = TT(T.ce[:, :], T.cb[:, 64:320], T.ha[:, 64:320], OP.add, tok["X6"], tok["Y6"], tok["X8"], tok["Y8"])
-        elif n == "OFF":
-            x = [None] * 4
-            for i in range(4):
-                x[i] = TT(T.off[:, 64 * i:64 * i + 64], T.ha[:, 64 * i + 64:64 * i + 128], q4, OP.add, tok["q4"], tok["Y8"])
-                if i >= 2:
-                    h = i - 2
-                    t_l1[h] = CP(T.l1[:, 128 * h:128 * h + 128], T.off[:, 128 * h:128 * h + 128], x[2 * h + 1])
-        elif n == "cmz":
-            tok[n] = FILL(T.cm[:, 0:W1], 0.0)
-        elif n == "vf" and vfills:
-            x0, x1, c = vfills.pop(0)
-            regions.append((x0, x1, FILL(T.fw[:, c:c + x1 - x0], 1.0)))
-
-    fills = []
-    c0 = V_FILL
-    while c0 < 4 * M - SRC - V_LATE - sum(P_FILL):
-        c1 = min(4 * M - SRC - V_LATE - sum(P_FILL), (c0 // 1024 + 1) * 1024)
-        fills.append((c0, c1))
-        c0 = c1
-    t_ev = [None] * len(PP)
+            return TS(T.og[:, c], T.cw[:, :], lim, OP.is_ge, T.psr[:, 4 + j:5 + j], OP.mult, tok["cw"], tok["psr"])
+        if n[0] == "o":
+            return TT(T.off[:, c], q4, T.ha[:, 64 * j + 64:64 * j + 128], OP.add, tok["q4"], tok["XY"[j // 2] + "8"])
+        if n == "ceX":
+            return TT(T.ce[:, 0:128], cb["X"], T.ha[:, 64:192], OP.add, tok["X8"])
+        if n == "ceY":
+            return TT(T.ce[:, 128:256], cb["Y"], T.ha[:, 192:320], OP.add, tok["Y8"])
+        if n[0] == "m":
+            return TT(T.xi[:, c], T["ps%d" % j][:, 256:320], T.ce[:, c], OP.min, tok["T%d" % j], tok["ce" + "XY"[j // 2]])
+        if n[0] == "a":
+            return TS(T.ai[:, c], T.xi[:, c], M - 1, OP.bitwise_and, None, None, tok["m%d" % j])
+        if n[0] == "c":
+            return TT(T.cc[:, c], q4, T.ai[:, c], OP.add, tok["a%d" % j])
+        if n[0] == "i":
+            return TS(T.l2[:, c], T.cc[:, c], 0.5, OP.mult, -0.25, OP.add, tok["c%d" % j])
+        if n[0] == "b":
+            return TS(T.ah[:, c], T.xi[:, c], 1, OP.bitwise_and, None, None, tok["m%d" % j])
+        if n[0] == "w" and n != "w01":
+            return TS(T.mh[:, c], T.ah[:, c], -15.0, OP.mult, 16.0, OP.add, tok["b%d" % j])
+        if n[0] == "d":
+            return TT(T.psv[:, c], T.ai[:, 64 * j + 64:64 * j + 128], T.ai[:, c], OP.subtract, *toks("a%d" % j, "a%d" % (j + 1)))
+        if n[0] == "n":
+            return TT(T.vi[:, c], T["ps%d" % j][:, 384:448], T.mh[:, c], OP.mult, tok["H%d" % j], tok["w%d" % j])
+        if n[0] == "s":
+            return TS(T.vb[:, c], T.vi[:, c], 4 + rank, OP.arith_shift_right, 1, OP.bitwise_and, tok["n%d" % j])
+        if n == "u0":
+            return TT(T.uu[:, 0:64], T.psv[:, 0:64], T.vb[:, 0:64], OP.mult, tok["s0"], tok["d0"])
+        if n == "first":
+            return TT(first, T.uu[:, 0:64], T.cc[:, 0:64], OP.add, tok["u0"], tok["c0"])
+        if n == "w01":
+            return TT(T.uu[:, 192:256], T.vb[:, 0:64], T.vb[:, 64:128], OP.mult, tok["s0"], tok["s1"])
+        if n == "u1":
+            return TT(T.uu[:, 64:128], T.psv[:, 64:128], T.uu[:, 192:256], OP.mult, tok["w01"], tok["d1"])
+        if n == "rest":
+            return TT(rest, T.psv[:, 128:192], T.uu[:, 192:256], OP.mult, tok["w01"], tok["d2"])
+        if n == "keep":
+            return TT(keep, first, T.uu[:, 64:128], OP.add, tok["u1"], tok["first"])
+        if n == "u2":
+            return TT(T.uu[:, 128:192], rest, T.vb[:, 128:192], OP.mult, tok["s2"], tok["rest"])
+        if n == "x":
+            return TT(T.xx[:, :], keep, T.uu[:, 128:192], OP.add, tok["u2"], tok["keep"])
+        return CP(T.l3[:, :], T.xx[:, :], tok["x"])
 
     def aop(n):
-        if n == "fill":
-            c0, c1 = fills.pop(0)
-            c = col(c0)
-            regions.append((c0, c1, COPY(T.fw[:, c:c + c1 - c0], T.fw[:, cs:cs + c1 - c0], 1.0, t_src)))
-        elif n == "id4":
-            tok[n] = COPY(T.id4k[:, :], T.idt[:, :], float(M), t_id)
-        elif n[0] == "e":
-            j = int(n[1])
-            x0, x1, bank, grp = PP[j]
-            ps = T[bank][:, 0:x1 - x0]
-            need("t", [ld_sn[grp], t_id, t_id6])
-            t.matmul(ps, T.idt[:, :], T.sr[:, 2 * x0:2 * x1:2], True, False)
-            x = done("t", t.matmul(ps, T.id16[:, :], T.sr[:, 2 * x0 + 1:2 * x1:2], False, True))
-            t_ev[j] = COPY(T.sw[:, H * rank + x0:H * rank + x1], ps, 1.0, x)
-        elif n == "xs":
-            SQUARE(T.psk[:, 0:64], T.cb[:, 0:64], 1.0, 0.0, tok["XO"])
-            tok["Xs"] = SQUARE(T.psk[:, 64:192], T.cb[:, 64:192], 1.0 / (2 * M), 2047.5, tok["X6"])
-        elif n == "ys":
-            tok["Ys"] = SQUARE(sq["Y"], T.cb[:, 192:320], 1.0 / (2 * M), 2047.5, tok["Y6"])
+        if ":" in n:
+            return look("a", n)
+        if n[0] in "XY":
+            return hash_step(n[0], n[1])
+        if n == "id4":
+            return COPY(T.id4k[:, :], T.idt[:, :], float(M), t_id)
+        if n == "id16":
+            return COPY(T.id16[:, :], T.idt[:, :], 16.0, t_id)
+        j = int(n[1])
+        x0, x1, grp = PP[j]
+        return COPY(T.sw[:, H * rank + x0:H * rank + x1], T["ps%d" % j][:, 0:x1 - x0], 1.0, tok["p%d" % j])
 
-    av = list(A_ORDER)
-    ready = {"xs": ["X6", "XO"], "ys": ["Y6"]}
-
-    def a_next():
-        while av and all([x in tok for x in ready.get(av[0], [])]):
-            n = av.pop(0)
-            if n != "fill" or fills:
-                aop(n)
-
-    a_next()
-    for n in V_ORDER:
-        vop(n)
-        if n == "r1":
-            need("t", [tok["r0"], tok["r1"], t_gs])
-            tok["psr"] = done("t", t.matmul(T.psr[:, 0:11], T.gs[:, :], T.rkf[:, 0:11], True, True))
-        if n == "g6":
-            need("t", [tok["og"], tok["id4"]])
-            for j in range(7):
-                ins = t.matmul(q4, T.id4k[:, :], T.og[:, 64 * j:64 * j + 64], j == 0, j == 6)
-            tok["q4"] = done("t", ins)
-        a_next()
-    while fills:
-        aop("fill")
-    while vfills:
-        vop("vf")
-    t_ce, t_zero = tok["ce"], tok["cmz"]
-
-    def s_parts(k):
-        q = (rank + k) % 4
-        lo, hi = M * q, M * q + M
-        deps = [tk for (x0, x1, tk) in regions if x0 < M * k + M and M * k < x1]
-        deps += [t_p[2]] if k == 0 else [("aft%d" % q, 3 * len(topo.engines(T.cores[q], core)))]
-        for f in range(3):
-            x = T.ft[:, 256 * f:256 * f + 256] if k == 0 else T.fl[3 * q + f]
-            tok["fx"] = dma("s", T.fw[f::16, lo:hi], x, "fx", *deps)
-
-    wm = T.cm[:, W1 + 15:W1 + 143:16]
-
-    def p_hist(j):
-        need("p", [t_ev[i] for i in range(len(PP)) if PP[i][3] == j])
-        lr[0] += send([hc], T.sw, hp[j][0], hp[j][1], "hs%d" % j)
-
-    def p_part(f):
-        need("p", [t_p[f]])
-        lr[0] += spread(g, T, topo, core, others, T.ft[:, 256 * f:256 * f + 256], "aft%d" % rank, T.fl[3 * rank + f])
-
-    def p_fill(j):
-        y = 4 * M - SRC - V_LATE - sum(P_FILL[j:])
-        for y0, y1, c in blocks(y, y + P_FILL[j]):
-            regions.append((y0, y1, CONST(T.fw[:, c:c + y1 - y0], [[0, y1 - y0]], 1)))
-
-    def p_w(j):
-        x = SEL(wm, T.on[:, 0:8], [[-16, 8]], OP.is_ge, 0, 1, t_w0)
-        tok["w"] = SEL(wm, wm, [[16, 8]], OP.is_ge, 2, -1, x)
-
-    def p_con(j):
-        tok["con"] = SEL(T.cm[:, 0:2048:16], T.o16[:, :], [[-1, 16], [-16, 8]], OP.is_equal, 0, 1, t_zero)
-
-    calls = {"h": p_hist, "t": p_part, "v": p_vec, "p": p_fill, "w": p_w, "con": p_con, "f": s_parts}
-
-    def call(n):
-        if n in calls:
-            calls[n](0)
+    def top(n):
+        if n == "psr":
+            return done("t", group(T.psr[:, 0:11], [(T.gs[:, :], T.rkf[:, 0:11])], *toks("r0", "r1", "gs")))
+        if n == "q4":
+            return done("t", group(q4, [(T.id4k[:, :], T.og[:, 64 * j:64 * j + 64]) for j in range(7)], *toks("g6", "id4")))
+        i = int(n[1])
+        ps = T["ps%d" % i]
+        if n[0] == "p":
+            x0, x1 = b0 + 2 * PP[i][0], b0 + 2 * PP[i][1]
+            ins = group(ps[:, 0:(x1 - x0) // 2], [(T.idt[:, :], T.fw[:, x0:x1:2]), (T.id16[:, :], T.fw[:, x0 + 1:x1:2])],
+                        tok[["ls%d" % j for j, (y0, y1) in enumerate(SP) if y0 <= PP[i][0] < y1][0]], t_id, tok["id16"])
+        elif n[0] == "H":
+            ins = group(ps[:, 384:448], [(T.cm[:, 127 * u:127 * u + 128], T["gb%d" % i][:, u::16]) for u in range(16)],
+                        tok["con"], *tok["g" + n])
         else:
-            calls[n[0]](int(n[1:]))
+            ins = group(ps[:, 256:320], [(T.c0[:, 15 - u:143 - u], T["ga%d" % i][:, u::16]) for u in range(16)],
+                        tok["wt"], *(tok["g" + n] + toks(*moved)))
+        return done("t", ins)
 
-    todo = list(S_ORDER)
+    lr = [0]
 
-    def s_next():
-        n = todo.pop(0)
+    def send(dsts, x, sem, out, *deps):
+        need("p", deps)
+        lr[0] += spread(g, T, topo, core, dsts, x, sem, out)
+        return ("lr", lr[0])
+
+    def pop(n):
+        if ":" in n:
+            return look("p", n)
+        if n == "gs":
+            return SEL(T.gs[:, :], T.f8[:, :], [[-1, 8], [0, 16]], OP.is_equal, 0, 1, t_f8)
+        if n == "kc":
+            CONST(T.kc[:, 0:4], [[M, 4]], 0)
+            return CONST(T.kc[:, 4:8], [[-1, 4]], 0)
+        if n == "wt":
+            w = T.c0[:, 15:143:16]
+            x = SEL(w, T.on[:, 0:8], [[-16, 8]], OP.is_ge, 0, 1, t_w0)
+            return SEL(w, w, [[16, 8]], OP.is_ge, 2, -1, x)
+        if n == "con":
+            return SEL(T.cm[:, 0:2048:16], T.on[:, :], [[-1, 16], [-16, 8]], OP.is_equal, 0, 1, *tok["zeros"])
+        if n == "hold":
+            return need("p", tok["full3"])
+        j = int(n[1])
+        out, sem, way = piece(T, rank, n)
+        if n[0] == "t":
+            x, deps = T.ft[:, 256 * j:256 * j + 256], toks(("k2", "k4", "k5")[j])
+        else:
+            x, deps = out, toks(*["e%d" % i for i in range(len(PP)) if PP[i][2] == j]) if n[0] == "h" else toks("lv%d" % j)
+        if way == "s":
+            return send(others, x, sem, out, *deps)
+        if way == "n":
+            return send([hc], x, n, out, *deps)
+        send([helper_of(across(core, T, topo), T, topo)], x, n, out, *deps)
+        return send([c for c in others if topo.die(c) == topo.die(core)], x, sem, out)
+
+    def sop(n):
+        if n == "chosen":
+            return dma("s", T.chosen[:, :], T.xx[:, :], "st", tok["x"])
+        if n[0] == "y":
+            c0, c1 = [int(c) for c in n.split(":")[1:]]
+            deps = toks(*[m for m in V_ORDER + A_ORDER if m[:2] == "V0" and c0 <= int(m.split(":")[1]) < c1])
+            return dma("s", T.y[:, 16 * c0:16 * c1], T.yt[:, 16 * c0:16 * c1], "st", *deps)
+        if n[0] == "@":
+            return need("s", toks(n[1:]))
+        k = int(n[1])
         if n[0] == "v":
-            s_vec(int(n[1:]))
+            return s_vec(k)
+        if n[0] == "s":
+            return s_seen(k)
+        q = (rank + k) % 4
+        if k == 0:
+            deps = toks("k2", "k4", "k5", *packed)
         else:
-            call(n)
+            deps = tok["full%d" % k] + [("aft%d" % q, 3 * len(topo.engines(T.cores[q], core)))]
+        for f in range(3):
+            x = dma("s", T.fw[f::16, M * q:M * q + M], T.ft[:, 256 * f:256 * f + 256] if k == 0 else T.fl[3 * q + f], "fx", *deps)
+        return x
 
-    for n in P_ORDER:
-        while n[0] == "v" and ld_v[int(n[1:])] is None:
-            s_next()
-        call(n)
-    while todo:
-        s_next()
-
-    def diag(u):
-        return T.cm[:, W1 + 15 - u:W1 + 143 - u]
-
-    def gather(q, out, win, lst, *deps):
-        need(q, deps)
-        if q == "a":
-            return done("a", a.activation(out, win.indirect(lst), AF.Copy))
-        return done("v", v.tensor_copy(out, win.indirect(lst)))
-
-    G = [[], [], [], []]
-    E = [[], [], []]
-    d = [None] * 4
-    e = [None] * 3
-    w = [None] * 3
-    PT = [None] * 4
-    PH = [None] * 3
-    all_s = ("asn", 3 * len(hp) * ne)
-
-    def GA(q, i, c0, c1):
-        if c0 < c1:
-            G[i].append(gather(q, T["ga%d" % i][:, 16 * c0:16 * c1], T.fw[:, :], T.l1[:, 64 * i + c0:64 * i + c1],
-                               tok["fx"], t_l1[i // 2]))
-
-    def PE(i):
-        need("t", G[i] + [tok["w"]] + t_ev)
-        out = T["ps%d" % (i // 2)][:, 64 * (i % 2):64 * (i % 2) + 64]
-        for u in range(16):
-            ins = t.matmul(out, diag(u), T["ga%d" % i][:, u::16], u == 0, u == 15)
-        PT[i] = done("t", ins)
-
-    def HI(q, i, c0, c1):
-        if c0 < c1:
-            E[i].append(gather(q, T["gb%d" % i][:, 16 * c0:16 * c1], T.sw[:, :], T.l2[:, 64 * i + c0:64 * i + c1],
-                               all_s, e[i], *t_ev))
-
-    def PK(i):
-        need("t", E[i] + [tok["con"]])
-        for u in range(16):
-            ins = t.matmul(T[PB[i]][:, 256:320], T.cm[:, 127 * u:127 * u + 128], T["gb%d" % i][:, u::16], u == 0, u == 15)
-        PH[i] = done("t", ins)
-
-    def decide(j):
-        c = slice(128 * j, 128 * j + 128)
-        h = slice(128 * j, min(192, 128 * j + 128))
-        m = {}
-
-        def f0():
-            m[0] = TT(T.xi[:, c], T["ps%d" % j][:, 0:128], T.ce[:, c], OP.min, PT[2 * j + 1], t_ce)
-
-        def f1():
-            m[1] = TS(T.ai[:, c], T.xi[:, c], M - 1, OP.bitwise_and, None, None, m[0])
-
-        def f2(i):
-            ci = slice(64 * i, 64 * i + 64)
-            d[i] = TT(T.cc[:, ci], T.ai[:, ci], q4, OP.add, m[1])
-
-        def f3():
-            x = TS(T.l2[:, h], T.cc[:, h], 0.5, OP.mult, -0.25, OP.add, d[2 * j], d[2 * j + (j == 0)])
-            for i in range(2 * j, min(3, 2 * j + 2)):
-                e[i] = x
-
-        def f4():
-            m[4] = TS(T.ah[:, h], T.xi[:, h], 1, OP.bitwise_and, None, None, m[0])
-
-        def f5():
-            x = TS(T.mh[:, h], T.ah[:, h], -0.9375, OP.mult, 1.0, OP.add, m[4])
-            for i in range(2 * j, min(3, 2 * j + 2)):
-                w[i] = x
-
-        if j == 0:
-            return [f0, f1, lambda: f2(0), lambda: f2(1), f3], [f4, f5]
-        return [f0, f1, lambda: f2(2), f3], [lambda: f2(3), f4, f5]
-
-    def run(calls):
-        for f in calls:
-            f()
-
-    for i in range(4):
-        GA("a", i, 0, GT[i])
-        GA("v", i, GT[i], 64)
-        PE(i)
-    now, later = decide(0)
-    run(now)
-    HI("a", 0, 0, HA[0])
-    HI("a", 1, 0, HA[1])
-    run(later)
-    HI("v", 0, HA[0], 64)
-    PK(0)
-    now, later = decide(1)
-    run(now)
-    HI("v", 1, HA[1], 64)
-    PK(1)
-    HI("a", 2, 0, HA[2])
-    run(later)
-    HI("v", 2, HA[2], 64)
-    PK(2)
-
-    bit = 16 << rank
-
-    def has(i):
-        c = slice(64 * i, 64 * i + 64)
-        x = TT(T.vi[:, c], T[PB[i]][:, 256:320], T.mh[:, c], OP.mult, PH[i], w[i])
-        return T.vb[:, c], TS(T.vb[:, c], T.vi[:, c], bit, OP.bitwise_and, None, None, x)
-
-    x = TT(T.psv[:, 0:192], T.cc[:, 64:256], T.cc[:, 0:192], OP.subtract, *d)
-    for i in range(3):
-        x = TS(T.psv[:, 192 + 64 * i:256 + 64 * i], T.psv[:, 64 * i:64 * i + 64], float(bit) ** (-1 - i), OP.mult, None, None, x)
-    t_dc = x
-    first, keep, rest = T.psr[:, 384:448], T.psr[:, 448:512], T.psk[:, 448:512]
-    b1, b2 = T.psk[:, 320:384], T.psk[:, 384:448]
-    s1, y = has(0)
-    x = TT(T.uu[:, 0:64], s1, T.psv[:, 192:256], OP.mult, y, t_dc)
-    t_b1 = TT(b1, s1, T.psv[:, 256:320], OP.mult)
-    t_b2 = TT(b2, s1, T.psv[:, 320:384], OP.mult)
-    x = TT(first, T.uu[:, 0:64], T.cc[:, 0:64], OP.add, x)
-    s2, y = has(1)
-    z = TT(T.uu[:, 64:128], s2, b1, OP.mult, y, t_b1)
-    t_r = TT(rest, s2, b2, OP.mult, t_b2)
-    t_k = TT(keep, T.uu[:, 64:128], first, OP.add, z, x)
-    s3, y = has(2)
-    y = TT(T.uu[:, 128:192], s3, rest, OP.mult, y, t_r)
-    t_x = TT(T.xx[:, :], T.uu[:, 128:192], keep, OP.add, y, t_k)
-    t_l3 = CP(T.l3[:, :], T.xx[:, :], t_x)
-    dma("s", T.chosen[:, :], T.xx[:, :], "st", t_x)
-
-    all_v = ("avc", 3 * len(VP) * ne)
-    yq = []
-    for c0, c1, q in YS:
-        yq.append((c0, c1, gather(q, T.yt[:, 16 * c0:16 * c1], T.vw[:, :], T.l3[:, c0:c1], all_v, t_l3, *ld_v)))
-    for c0, c1, x in yq:
-        t_st = dma("s", T.y[:, 16 * c0:16 * c1], T.yt[:, 16 * c0:16 * c1], "st", x)
+    queues = [(list(V_ORDER), vop), (list(A_ORDER), aop), (list(T_ORDER), top), (list(P_ORDER), pop), (list(S_ORDER), sop)]
+    while any([x for x, f in queues]):
+        made = 0
+        for x, f in queues:
+            while x:
+                try:
+                    r = f(x[0])
+                except KeyError:
+                    break
+                if r is not None:
+                    tok[x[0]] = r
+                made += 1
+                if x.pop(0)[0] == "F":
+                    break
+        assert made
 
     need("p", [("lr", lr[0])])
-    need("s", [t_st] + [(s, cnt[s]) for s in ("v", "a", "p", "t", "ldt", "lds", "ldr", "fx")])
-    need("s", ld_sn + ld_v)
+    need("s", [(s, cnt[s]) for s in cnt])

@@ -4,23 +4,23 @@ from concourse.mybir import AluOpType as OP, ActivationFunctionType as AF
 M, K = 4096, 64
 H = M // 2
 MID = 1 << 24
-WRAP = 64 * M
-TP = ["n", "n", "s"]
-HP = [(0, 512, "n"), (512, 1536, "n"), (1536, 2048, "f")]
-VP = [(0, 128, "n"), (128, 384, "s"), (384, 640, "n"), (640, 2176, "n"), (2176, 4096, "s")]
-HELPER_ORDER = "v0 t0 t1 h0 h1 h2 v2 v3".split()
+N1 = 1 << 23
+TP = ["s", "s", "s"]
+HP = [(0, 512, "n"), (512, 1536, "n"), (1536, 2048, "n")]
+VP = [(0, 256, "n"), (256, 1920, "n"), (1920, 4096, "s")]
+HELPER_ORDER = "v0 h0 h1 h2 v1".split()
 SP = [(0, 1024), (1024, 2048)]
 PP = [(0, 512, 0), (512, 1024, 1), (1024, 1536, 1), (1536, 2048, 2)]
-LOADS = "v0 d t r s0 v1 s1".split()
+LOADS = "d t v0 s0 r s1".split()
 SRC = 1024
-P_ORDER = "kc v0 Z:1024 v1 t0 gs t1 t2 h0 F:512 h1 h2 wt v2 v3 con v4".split()
-S_ORDER = "f0 f1 f2 f3 v2 v3 v4 chosen y:0:16 y:32:48 y:16:32 y:48:64".split()
-A_ORDER = ("F:1024 id16 F:256 Xc F:512 Yc F:256 X2 F:512 Y2 F:512 e0 id4 F:512 Xs e1 F:512 e2 Ys e3 F:768 F:512 "
-           "T0:0:30 T1:0:32 T2:0:40 T3:0:64 H0:0:40 H1:0:40 H2:0:34 V0:32:48 V0:48:64").split()
-V_ORDER = ("lo hi l64 F:256 th cf F:256 X0 Y0 X1 k0 F:256 Y1 k1 X4 k2 X5 k3 XO r0 F:256 X6 Y4 k4 F:768 k5 r1 Y5 X7 F:512 "
-           "am Y6 cw X8 g0 g1 g2 g3 g4 g5 g6 F:768 F:768 F:256 Y7 F:256 Y8 F:1024 o0 o1 o2 o3 Xl Yl Z:1024 ceX ceY "
-           "T0:30:64 T1:32:64 T2:40:64 m0 a0 b0 c0 w0 m1 i0 a1 b1 H0:40:48 w1 c1 H0:48:64 i1 m2 d0 a2 b2 H1:40:52 c2 w2 "
-           "H1:52:64 i2 d1 m3 H2:34:44 n0 a3 H2:44:64 s0 d2 u0 n1 first s1 w01 u1 rest keep n2 s2 u2 x l3 V0:0:16 V0:16:32").split()
+P_ORDER = "kc v0 F:256 t0 gs t1 t2 h0 F:1024 h1 h2 Z:768 wt v1 v2 Z:768 con".split()
+S_ORDER = "f0 f1 f2 f3 v1 v2 chosen y:0:18 y:34:50 y:18:34 y:50:64".split()
+A_ORDER = ("F:768 id16 F:1024 id4 F:768 X3 Y3 e0 e1 F:512 Xs Ys e2 e3 F:256 F:1024 "
+           "T0:0:30 T1:0:32 T2:0:40 T3:0:48 H0:0:40 H1:0:48 H2:0:40 V0:34:50 V0:50:64").split()
+V_ORDER = ("F:1024 F:1024 sdf hi k0 X0 cf k1 X1 Y0 k2 Y1 X2 k3 r0 Y2 k4 k5 X4 Y4 X5 r1 Y5 X6 Y6 F:768 F:1024 X7 Y7 am cw "
+           "F:1024 g0 Y8 g1 X8 g2 g3 g4 g5 F:768 g6 ceX Z:512 o0 o1 ceY o2 o3 Xl Yl "
+           "T0:30:64 T1:32:64 T2:48:64 m0 T2:40:48 a0 b0 c0 m1 T3:56:64 i0 b1 a1 T3:48:56 w0 c1 d0 w1 i1 m2 H0:40:64 a2 b2 "
+           "c2 w2 d1 m3 i2 H1:48:64 a3 n0 d2 s0 H2:40:64 u0 y1 y2 n1 first s1 u1 rest keep n2 s2 u2 x l3 V0:0:18 V0:18:34").split()
 T_ORDER = "p0 p1 p2 p3 psr q4 T0 T1 T2 T3 H0 H1 H2".split()
 
 SCRATCH = {
@@ -48,8 +48,7 @@ SCRATCH = {
     "c0": ("sbuf", [128, 144], "bfloat16"),
     "n1": ("sbuf", [128, 320], "int32"),
     "n2": ("sbuf", [128, 320], "int32"),
-    "c64": ("sbuf", [128, 320], "float32"),
-    "hx": ("sbuf", [128, 320], "float32"),
+    "hx": ("sbuf", [128, 320], "int32"),
     "hs": ("sbuf", [128, 320], "float32"),
     "hs2": ("sbuf", [128, 320], "int32"),
     "hb": ("sbuf", [128, 320], "int32"),
@@ -83,7 +82,7 @@ for _i in range(4):
 for _i in range(3):
     SCRATCH["gb%d" % _i] = ("sbuf", [128, 1024], "bfloat16")
 
-SEMAPHORES = ["v", "a", "p", "t", "ldt", "lds", "ldr", "fx", "st", "lr", "aft0", "aft1", "aft2", "aft3", "ah", "av"]
+SEMAPHORES = ["v", "a", "p", "t", "ldt", "lds", "ldr", "fd", "fx", "st", "lr", "aft0", "aft1", "aft2", "aft3", "ah", "av"]
 SEMAPHORES += ["%s%d" % (s, j) for s in ("sn", "t", "h", "vc", "v") for j in range(6)]
 
 
@@ -246,6 +245,8 @@ def rank_program(g, core, T, topo):
         out = T.fw[:, c:c + x1 - x0]
         if q == "v":
             r = FILL(out, 1.0)
+        elif q == "s":
+            r = dma("s", out, T.seen[:, 0:x1 - x0], "fd")
         elif q == "a":
             r = COPY(out, T.fw[:, cs:cs + x1 - x0], 1.0, t_src)
         else:
@@ -271,23 +272,19 @@ def rank_program(g, core, T, topo):
             tok["zeros"] = [r for n, r in zeros]
         return r
 
-    t_n1 = done("p", g.iota(T.n1[:, :], [[1597, 5], [5 * 1597, 64]], 0, 0))
+    t_n1 = done("p", g.iota(T.n1[:, :], [[1597, 5], [5 * 1597, 64]], -N1, 0))
     cs = (b0 - SRC) % (4 * M)
     t_on = FILL(T.on[:, :], 1.0)
     t_src = FILL(T.fw[:, cs:cs + SRC], 1.0)
     filled.append(t_src)
     t_f8 = FILL(T.f8[:, :], 1.0)
     t_id = SEL(T.idt[:, :], T.on[:, :], [[-1, 128]], OP.is_equal, 0, 1, t_on)
-    x = TS(T.n2[:, :], T.n1[:, :], M - 1, OP.bitwise_and, None, None, t_n1)
     t_w0 = FILL(T.c0[:, :], 0.0)
-    t_c64 = TS(T.c64[:, :], T.n2[:, :], 64.0, OP.mult, None, None, x)
 
     CH = {"X": (0, 192), "Y": (192, 320)}
     hl = {"X": T.psx[:, 0:192], "Y": T.psy[:, 0:128]}
-    raw = {"X": T.psx[:, 192:384], "Y": T.psy[:, 128:256]}
-    cb = {"X": T.psx[:, 384:512], "Y": T.psy[:, 256:384]}
-    ob = T.psx[:, 192:256]
-    l64, th, cf = [T.cf[:, j:j + 1] for j in range(3)]
+    cb = {"X": T.psx[:, 192:384], "Y": T.psy[:, 128:256]}
+    sdf, cf = T.cf[:, 0:1], T.cf[:, 1:2]
     pk, rp = T.psv[:, 0:256], T.psv[:, 256:512]
     q4 = T.psr[:, 64:128]
     packed = ["p%d" % j for j in range(len(PP))]
@@ -297,27 +294,22 @@ def rank_program(g, core, T, topo):
         c0, c1 = CH[f]
         c = slice(c0, c1)
         cc = slice(max(c0, 64), c1)
-        if s == "c":
-            return ACT(raw[f], T.c64[:, c], AF.Identity, 1.0, l64, t_c64, tok["l64"])
         if s == "0":
-            return TS(T.hx[:, c], T.c64[:, c], th, OP.is_ge, -float(WRAP), OP.mult, t_c64, tok["th"])
+            return TS(T.hx[:, c], T.n1[:, c], sdf, OP.add, 64.0, OP.mult, t_n1, tok["sdf"])
         if s == "1":
-            return TT(hl[f], raw[f], T.hx[:, c], OP.add, tok[f + "0"], tok[f + "c"])
+            return TS(T.n2[:, c], T.hx[:, c], 64 * 4095, OP.bitwise_and, None, None, tok[f + "0"])
         if s == "2":
-            return ACT(T.hs[:, c], hl[f], AF.Square, 1.0 / 64, 0.0, tok[f + "1"])
+            return CP(hl[f], T.n2[:, c], tok[f + "1"])
+        if s == "3":
+            return ACT(T.hs[:, c], hl[f], AF.Square, 1.0 / 64, 0.0, tok[f + "2"])
         if s == "4":
-            return TS(T.hs2[:, c], T.hs[:, c], cf, OP.add, None, None, tok[f + "2"], tok["cf"])
+            return TS(T.hs2[:, c], T.hs[:, c], cf, OP.add, None, None, tok[f + "3"], tok["cf"])
         if s == "5":
             return TS(T.hb[:, c], T.hs2[:, c], 6, OP.arith_shift_right, 4095, OP.bitwise_and, tok[f + "4"])
         if s == "6":
-            return TS(cb[f], T.hb[:, cc], float(2 * M), OP.mult, float(M - MID), OP.add, tok[f + "5"])
-        if s == "O":
-            return CP(ob, T.hb[:, 0:64], tok[f + "5"])
+            return TS(cb[f], T.hb[:, c], float(2 * M), OP.mult, float(M - MID), OP.add, tok[f + "5"])
         if s == "s":
-            x = tok[f + "6"]
-            if f == "X":
-                ACT(T.sq[:, 0:64], ob, AF.Square, 1.0, 0.0, tok["XO"], x)
-            return ACT(T.sq[:, cc], cb[f], AF.Square, 1.0 / (2 * M), 2047.5, x)
+            return ACT(T.sq[:, c], cb[f], AF.Square, 1.0 / (2 * M), 2047.5, tok[f + "6"])
         if s == "7":
             return TT(T.ht2[:, c], hl[f], T.sq[:, c], OP.add, tok[f + "s"])
         if s == "8":
@@ -354,12 +346,8 @@ def rank_program(g, core, T, topo):
             return look("v", n)
         if n[0] in "XY":
             return hash_step(n[0], n[1])
-        if n == "lo":
-            return TS(T.col[:, 0:1], T.sdi[:, :], M - 1, OP.bitwise_and, None, None, ld_s)
-        if n == "l64":
-            return TS(l64, T.col[:, 0:1], 64.0, OP.mult, None, None, tok["lo"])
-        if n == "th":
-            return TS(th, T.col[:, 0:1], -64.0, OP.mult, float(WRAP), OP.add, tok["lo"])
+        if n == "sdf":
+            return CP(sdf, T.sdi[:, :], ld_s)
         if n == "hi":
             return TS(T.col[:, 1:2], T.sdi[:, :], 6, OP.logical_shift_right, 64 * 4095, OP.bitwise_and, ld_s)
         if n == "cf":
@@ -383,14 +371,14 @@ def rank_program(g, core, T, topo):
         if n == "am":
             return TS(T.am[:, :], T.ht2[:, 0:64], 4, OP.arith_shift_right, 12288, OP.bitwise_and, tok["X7"])
         if n == "cw":
-            return TT(T.cw[:, :], ob, T.am[:, :], OP.add, tok["am"])
+            return TT(T.cw[:, :], T.hb[:, 0:64], T.am[:, :], OP.add, tok["am"])
         if n[0] == "g":
             lim = T.psr[:, j:j + 1] if j < 4 else float(M * (j - 3))
             return TS(T.og[:, c], T.cw[:, :], lim, OP.is_ge, T.psr[:, 4 + j:5 + j], OP.mult, tok["cw"], tok["psr"])
         if n[0] == "o":
             return TT(T.off[:, c], q4, T.ha[:, 64 * j + 64:64 * j + 128], OP.add, tok["q4"], tok["XY"[j // 2] + "8"])
         if n == "ceX":
-            return TT(T.ce[:, 0:128], cb["X"], T.ha[:, 64:192], OP.add, tok["X8"])
+            return TT(T.ce[:, 0:128], T.psx[:, 256:384], T.ha[:, 64:192], OP.add, tok["X8"])
         if n == "ceY":
             return TT(T.ce[:, 128:256], cb["Y"], T.ha[:, 192:320], OP.add, tok["Y8"])
         if n[0] == "m":
@@ -403,7 +391,7 @@ def rank_program(g, core, T, topo):
             return TS(T.l2[:, c], T.cc[:, c], 0.5, OP.mult, -0.25, OP.add, tok["c%d" % j])
         if n[0] == "b":
             return TS(T.ah[:, c], T.xi[:, c], 1, OP.bitwise_and, None, None, tok["m%d" % j])
-        if n[0] == "w" and n != "w01":
+        if n[0] == "w":
             return TS(T.mh[:, c], T.ah[:, c], -15.0, OP.mult, 16.0, OP.add, tok["b%d" % j])
         if n[0] == "d":
             return TT(T.psv[:, c], T.ai[:, 64 * j + 64:64 * j + 128], T.ai[:, c], OP.subtract, *toks("a%d" % j, "a%d" % (j + 1)))
@@ -415,12 +403,12 @@ def rank_program(g, core, T, topo):
             return TT(T.uu[:, 0:64], T.psv[:, 0:64], T.vb[:, 0:64], OP.mult, tok["s0"], tok["d0"])
         if n == "first":
             return TT(first, T.uu[:, 0:64], T.cc[:, 0:64], OP.add, tok["u0"], tok["c0"])
-        if n == "w01":
-            return TT(T.uu[:, 192:256], T.vb[:, 0:64], T.vb[:, 64:128], OP.mult, tok["s0"], tok["s1"])
+        if n[0] == "y":
+            return TT(T.psv[:, 320 + 64 * j:384 + 64 * j], T.psv[:, c], T.vb[:, 0:64], OP.mult, tok["s0"], tok["d%d" % j])
         if n == "u1":
-            return TT(T.uu[:, 64:128], T.psv[:, 64:128], T.uu[:, 192:256], OP.mult, tok["w01"], tok["d1"])
+            return TT(T.uu[:, 64:128], T.psv[:, 384:448], T.vb[:, 64:128], OP.mult, tok["s1"], tok["y1"])
         if n == "rest":
-            return TT(rest, T.psv[:, 128:192], T.uu[:, 192:256], OP.mult, tok["w01"], tok["d2"])
+            return TT(rest, T.psv[:, 448:512], T.vb[:, 64:128], OP.mult, tok["s1"], tok["y2"])
         if n == "keep":
             return TT(keep, first, T.uu[:, 64:128], OP.add, tok["u1"], tok["first"])
         if n == "u2":
@@ -434,6 +422,10 @@ def rank_program(g, core, T, topo):
             return look("a", n)
         if n[0] in "XY":
             return hash_step(n[0], n[1])
+        if n == "k2":
+            return COPY(T.ft[:, 0:256], pk, 1.0, tok["k1"])
+        if n == "k4":
+            return COPY(T.ft[:, 256:512], rp, 1.0, tok["k3"])
         if n == "id4":
             return COPY(T.id4k[:, :], T.idt[:, :], float(M), t_id)
         if n == "id16":
@@ -491,7 +483,7 @@ def rank_program(g, core, T, topo):
         else:
             x, deps = out, toks(*["e%d" % i for i in range(len(PP)) if PP[i][2] == j]) if n[0] == "h" else toks("lv%d" % j)
         if way == "s":
-            return send(others, x, sem, out, *deps)
+            return send(others[::-1] if n[0] == "t" else others, x, sem, out, *deps)
         if way == "n":
             return send([hc], x, n, out, *deps)
         send([helper_of(across(core, T, topo), T, topo)], x, n, out, *deps)
@@ -504,6 +496,8 @@ def rank_program(g, core, T, topo):
             c0, c1 = [int(c) for c in n.split(":")[1:]]
             deps = toks(*[m for m in V_ORDER + A_ORDER if m[:2] == "V0" and c0 <= int(m.split(":")[1]) < c1])
             return dma("s", T.y[:, 16 * c0:16 * c1], T.yt[:, 16 * c0:16 * c1], "st", *deps)
+        if n[0] == "F":
+            return look("s", n)
         if n[0] == "@":
             return need("s", toks(n[1:]))
         k = int(n[1])

@@ -5,24 +5,54 @@ M, K = 4096, 64
 H = M // 2
 MID = 1 << 24
 N1 = 1 << 23
+NB = 4
+SYM = 0
+CH = {"X": (0, 192), "Y": (192, 320)}
 TP = ["s", "s", "s"]
 HP = [(0, 512, "n"), (512, 1536, "n"), (1536, 2048, "n")]
 VP = [(0, 256, "n"), (256, 1920, "n"), (1920, 4096, "s")]
 HELPER_ORDER = "v0 h0 h1 h2 v1".split()
 SP = [(0, 1024), (1024, 2048)]
 PP = [(0, 512, 0), (512, 1024, 1), (1024, 1536, 1), (1536, 2048, 2)]
-LOADS = "d t v0 s0 r s1".split()
 SRC = 1024
-P_ORDER = "kc v0 F:256 t0 gs t1 t2 h0 F:1024 h1 h2 Z:768 wt v1 v2 Z:768 con".split()
+LOADS = "d t v0 s0 r s1".split()
+P_ORDER = "kc v0 F:256 t0 gs t1 t2 h0 F:1024 h1 h2 Z:768 wt0 v1 v2 Z:768 con".split()
 S_ORDER = "f0 f1 f2 f3 v1 v2 chosen y:0:18 y:34:50 y:18:34 y:50:64".split()
 A_ORDER = ("F:768 id16 F:1024 id4 F:768 X3 Y3 e0 e1 F:512 Xs Ys e2 e3 F:256 F:1024 "
            "T0:0:30 T1:0:32 T2:0:40 T3:0:48 H0:0:40 H1:0:48 H2:0:40 V0:34:50 V0:50:64").split()
 V_ORDER = ("F:1024 F:1024 sdf hi k0 X0 cf k1 X1 Y0 k2 Y1 X2 k3 r0 Y2 k4 k5 X4 Y4 X5 r1 Y5 X6 Y6 F:768 F:1024 X7 Y7 am cw "
            "F:1024 g0 Y8 g1 X8 g2 g3 g4 g5 F:768 g6 ceX Z:512 o0 o1 ceY o2 o3 Xl Yl "
            "T0:30:64 T1:32:64 T2:48:64 m0 T2:40:48 a0 b0 c0 m1 T3:56:64 i0 b1 a1 T3:48:56 w0 c1 d0 w1 i1 m2 H0:40:64 a2 b2 "
-           "c2 w2 d1 m3 i2 H1:48:64 a3 n0 d2 s0 H2:40:64 u0 y1 y2 n1 first s1 u1 rest keep n2 s2 u2 x l3 V0:0:18 V0:18:34").split()
+           "c2 w2 d1 m3 i2 H1:48:64 a3 n0 d2 s0 z0 H2:40:64 n1 s1 n2 s2 scan l3 x V0:0:18 V0:18:34").split()
 T_ORDER = "p0 p1 p2 p3 psr q4 T0 T1 T2 T3 H0 H1 H2".split()
-
+CH = {"W": (0, 64), "X": (64, 192), "Y": (192, 320)}
+P_ORDER = 'kc gs v0 t0 wa t1 wb t2 h0 F2:512 h1 h2 F3:512 Z:768 v1 v2 Z:768 con'.split()
+S_ORDER = 'f0 f1 f2 f3 v1 v2 chosen y:0:34 y:34:64'.split()
+A_ORDER = 'F1:1024 id16 F2:512 F1:768 F2:512 id4 F2:512 e0 e1 Y3 F1:256 X3 e2 e3 F3:768 Xs Ys T0:0:32 T1:0:34 T2:0:34 T3:0:44 H0:0:46 H1:0:42 H2:0:30 x V0:18:34 V0:50:64'.split()
+V_ORDER = 'F1:1024 F1:1024 sdf hi k0 W0 X0 Y0 W1 k1 X1 cf W3 k2 r0 W4 Y1 k3 X2 W5 k4 Ws Y2 k5 W7 F2:1024 r1 am F2:1024 X4 cw Y4 X5 g3 g2 Y5 F3:768 X6 Y6 F3:1024 g6 g1 g0 X7 g5 g4 Y7 X8 Z:512 Y8 o1 o0 o2 o3 Xl ceX Yl T0:32:64 T1:34:64 T2:34:54 ceY m0 T2:54:64 a0 b0 m1 c0 T3:58:64 a1 i0 T3:44:58 m2 c1 b1 a2 i1 H0:46:64 c2 b2 z0 i2 H1:42:64 H2:30:64 m3 w1 w0 d0 a3 w2 n0 d1 n1 d2 n2 s1 s0 s2 scan l3 V0:0:18 V0:34:50'.split()
+T_ORDER = 'p0 p1 p2 p3 psr q4 T0 T1 T2 T3 H0 H1 H2'.split()
+CH = {"X": (0, 192), "Y": (192, 320)}
+P_ORDER = 'kc gs v0 t0 wa t1 wb t2 h0 F3:512 h1 h2 Z:1024 Z:512 con v1 v2'.split()
+S_ORDER = 'F1:2048 f0 f1 f2 f3 @T0:34:64 v1 v2 chosen y:0:34 y:34:64'.split()
+A_ORDER = 'F1:512 id16 Xh Xw k2 X3 F3:512 k4 e0 Y3 F2:512 Xs e1 e2 e3 Ys id4 T0:0:34 T1:0:26 T2:0:38 T3:0:44 H0:0:42 H1:0:36 H2:0:32 x V0:18:34 V0:50:64'.split()
+V_ORDER = 'F2:512 lo F2:512 sdf F2:512 k0 F1:512 k1 F2:512 F3:512 r0 cf k3 F1:512 X4 r1 F2:512 X5 k5 X6 F2:512 F3:512 Y4 F1:512 F3:512 X7 F2:512 am F3:512 X8 Y5 z1 cw Y6 g3 g6 g2 g1 g4 g0 g5 ceX Y7 Z:512 Y8 o0 o1 o2 o3 Xl Yl ceY T0:34:64 T1:26:64 T2:38:56 m0 T2:56:64 a0 T3:44:58 c0 m1 T3:58:64 i0 a1 b0 m2 b1 c1 a2 b2 i1 c2 H0:42:64 i2 H1:36:64 H2:32:64 m3 w0 d0 w1 d1 a3 n1 n0 w2 d2 s0 n2 s1 s2 scan l3 V0:0:18 V0:34:50'.split()
+T_ORDER = 'Xa Ya Xb Yb p0 p1 psr p2 p3 q4 T0 T1 T2 T3 H0 H1 H2'.split()
+SYM = 1
+HP = [(0, 1024, "n"), (1024, 2048, "n")]
+PP = [(0, 512, 0), (512, 1024, 0), (1024, 1536, 1), (1536, 2048, 1)]
+VP = [(0, 256, 'n'), (256, 832, 'n'), (832, 2496, 'n'), (2496, 4096, 's')]
+HELPER_ORDER = 'v0 v1 h0 h1 v2'.split()
+P_ORDER = 'gs kc v0 wa t0 t1 v1 t2 h0 F3:512 wb h1 Z:1024 v2 v3 Z:512 con'.split()
+S_ORDER = 'v1 f0 f1 f2 f3 v2 v3 chosen y:0:34 y:34:64'.split()
+A_ORDER = 'F2:512 F1:512 id16 Xh Xw k2 F2:512 X3 k4 e0 F2:512 e1 Xs Y3 e2 F3:512 e3 Ys id4 T0:0:22 T1:0:34 T2:0:42 T3:0:60 H0:0:42 H1:0:24 H2:0:38 x V0:18:34 V0:50:64'.split()
+V_ORDER = 'F2:512 lo F2:512 sdf k0 F3:512 k1 F1:512 F1:512 F2:512 F1:512 k3 F1:512 cf F1:512 F1:512 F3:512 X4 r0 k5 X5 r1 X6 F2:512 F2:512 F3:512 Y4 X7 F1:512 X8 Y5 am ceX F3:512 cw Y6 g6 g0 g2 g4 g1 g3 g5 z1 Y7 Z:512 Y8 o0 o1 o3 Xl o2 ceY Yl T0:22:64 T1:34:64 T2:46:64 m0 T2:42:46 a0 b0 T3:60:62 m1 c0 T3:62:64 b1 a1 i0 w1 m2 w0 c1 a2 b2 i1 c2 H0:42:64 i2 H1:24:64 m3 H2:38:64 w2 n0 n1 a3 d0 s1 d2 s0 n2 d1 s2 scan l3 V0:0:18 V0:34:50'.split()
+T_ORDER = 'Xa Xb p0 p1 p2 Ya Yb psr p3 q4 T0 T1 T2 T3 H0 H1 H2'.split()
+P_ORDER = 'gs z2 v0 t0 kc t1 v1 wa t2 h0 F2:512 h1 wb Z:512 Z:1024 v2 v3 Z:512 con'.split()
+S_ORDER = 'v1 f0 f2 f1 f3 v2 v3 chosen y:0:34 y:34:64'.split()
+A_ORDER = 'F1:512 F3:512 Xh id16 Xw F1:512 X3 k4 Y3 e0 e1 Xs e2 e3 F3:512 F3:512 id4 Ys T0:0:30 T1:0:40 T2:0:28 T3:0:50 H0:0:46 H1:0:36 H2:0:30 x V0:18:34 V0:50:64'.split()
+V_ORDER = 'F2:512 lo F2:512 sdf k0 F2:512 k1 F1:512 k2 cf F3:512 k3 F2:512 F1:512 F2:512 X4 k5 X5 F3:512 X6 F1:512 F2:512 r0 F1:512 X7 Y4 F2:512 F3:512 am r1 Y5 F1:512 cw F1:512 g3 Y6 g5 g2 g0 g1 g4 g6 Y7 X8 Y8 o1 o0 o2 o3 Xl ceX Yl ceY T0:30:64 T1:40:64 T2:28:58 m0 T2:58:64 a0 T3:50:60 c0 b0 m1 i0 T3:60:64 a1 m2 b1 c1 a2 w0 i1 d0 c2 H0:46:64 i2 H1:36:64 H2:30:64 m3 n0 b2 a3 w1 s0 w2 d2 n1 n2 d1 s1 s2 scan l3 V0:0:18 V0:34:50'.split()
+T_ORDER = 'Xa Ya Xb Yb p0 p1 p2 p3 psr q4 T0 T1 T2 T3 H0 H1 H2'.split()
+VP = [(0, 256, 'n'), (256, 704, 'n'), (704, 2112, 'n'), (2112, 4096, 's')]
 SCRATCH = {
     "fw": ("sbuf", [128, 4 * M], "bfloat16"),
     "sw": ("sbuf", [128, 4 * H], "bfloat16"),
@@ -45,8 +75,14 @@ SCRATCH = {
     "id4k": ("sbuf", [128, 128], "bfloat16"),
     "id16": ("sbuf", [128, 128], "bfloat16"),
     "cm": ("sbuf", [128, 2048], "bfloat16"),
-    "c0": ("sbuf", [128, 144], "bfloat16"),
+    "c0": ("sbuf", [128, 272], "bfloat16"),
+    "pen": ("sbuf", [128, 128], "bfloat16"),
+    "mt": ("sbuf", [128, 256], "float32"),
     "n1": ("sbuf", [128, 320], "int32"),
+    "nf": ("sbuf", [128, 320], "float32"),
+    "hf": ("sbuf", [128, 320], "float32"),
+    "hw": ("sbuf", [128, 320], "bfloat16"),
+    "f64": ("sbuf", [1, 128], "float32"),
     "n2": ("sbuf", [128, 320], "int32"),
     "hx": ("sbuf", [128, 320], "int32"),
     "hs": ("sbuf", [128, 320], "float32"),
@@ -56,7 +92,8 @@ SCRATCH = {
     "ht2": ("sbuf", [128, 320], "int32"),
     "ha": ("sbuf", [128, 320], "int32"),
     "ce": ("sbuf", [128, 256], "float32"),
-    "off": ("sbuf", [128, 256], "float32"),
+    "off": ("sbuf", [128, 256], "int32"),
+    "of2": ("sbuf", [128, 256], "int32"),
     "l1": ("sbuf", [128, 256], "uint16"),
     "l2": ("sbuf", [128, 192], "uint16"),
     "l3": ("sbuf", [128, 64], "uint16"),
@@ -68,6 +105,8 @@ SCRATCH = {
     "vi": ("sbuf", [128, 192], "int32"),
     "vb": ("sbuf", [128, 192], "int32"),
     "uu": ("sbuf", [128, 256], "float32"),
+    "sf": ("sbuf", [128, 256], "int32"),
+    "so": ("sbuf", [128, 256], "float32"),
     "xx": ("sbuf", [128, 64], "float32"),
     "yt": ("sbuf", [128, 1024], "bfloat16"),
     "on": ("sbuf", [128, 128], "bfloat16"),
@@ -114,6 +153,15 @@ def across(core, T, topo):
     return [c for c in T.cores if c not in mine][mine.index(core)]
 
 
+def turn(core, T, topo):
+    if not SYM:
+        return after(T, T.rank_of(core))
+    a = across(core, T, topo)
+    far = [a] + [c for c in T.cores if topo.die(c) == topo.die(a) and c != a]
+    near = [c for c in T.cores if topo.die(c) == topo.die(core) and c != core]
+    return far + near if SYM == 1 else near + far
+
+
 def piece(T, r, n):
     if n[0] == "t":
         return T.fl[3 * r + int(n[1])], "aft%d" % r, TP[int(n[1])]
@@ -128,7 +176,7 @@ def helper_program(g, core, T, topo, near):
     for name in HELPER_ORDER:
         way = piece(T, 0, name)[2]
         if way == "n":
-            owner, dsts = near, after(T, T.rank_of(near))
+            owner, dsts = near, turn(near, T, topo)
         else:
             owner, dsts = far, [c for c in after(T, T.rank_of(far)) if topo.die(c) == topo.die(core)]
         x, sem, way = piece(T, T.rank_of(owner), name)
@@ -145,10 +193,13 @@ def rank_program(g, core, T, topo):
                 helper_program(g, core, T, topo, c)
         return
 
-    others = after(T, rank)
+    others = turn(core, T, topo)
+    owners = [rank] + [T.rank_of(c) for c in others]
     hc = helper_of(core, T, topo)
     ne = len(topo.engines(core, hc))
     b0 = M * rank
+    bs = b0 if NB == 4 else M * (1 - rank % 2)
+    cs = (bs - SRC) % (NB * M) if NB == 2 else M * owners[3] + M - SRC
     engs = {"v": g.vector, "a": g.scalar, "p": g, "t": g.tensor, "s": g.sync}
     cnt = {}
     seen = {k: {} for k in engs}
@@ -185,6 +236,10 @@ def rank_program(g, core, T, topo):
         need("v", deps)
         return done("v", v.tensor_copy(out, x))
 
+    def SCAN(out, x, y, *deps):
+        need("v", deps)
+        return done("v", v.tensor_tensor_scan(out, x, y, 0.0, OP.mult, OP.add))
+
     def FILL(ap, c):
         return done("v", v.memset(ap, c))
 
@@ -219,7 +274,7 @@ def rank_program(g, core, T, topo):
 
     def s_seen(j):
         x0, x1 = SP[j]
-        tok["ls%d" % j] = dma("s", T.fw[:, b0 + 2 * x0:b0 + 2 * x1], T.seen[:, 2 * x0:2 * x1], "sn%d" % j)
+        tok["ls%d" % j] = dma("s", T.fw[:, bs + 2 * x0:bs + 2 * x1], T.seen[:, 2 * x0:2 * x1], "sn%d" % j)
 
     for n in LOADS:
         if n[0] == "v":
@@ -241,20 +296,41 @@ def rank_program(g, core, T, topo):
         x0 = upto[0]
         x1 = min(x0 + w, (x0 // M + 1) * M)
         upto[0] = x1
-        c = (b0 + x0) % (4 * M)
+        c = (bs + x0) % (NB * M)
         out = T.fw[:, c:c + x1 - x0]
         if q == "v":
             r = FILL(out, 1.0)
-        elif q == "s":
-            r = dma("s", out, T.seen[:, 0:x1 - x0], "fd")
         elif q == "a":
             r = COPY(out, T.fw[:, cs:cs + x1 - x0], 1.0, t_src)
         else:
             r = CONST(out, [[0, x1 - x0]], 1)
         filled.append(r)
-        if x1 % M == 0 or x1 == 4 * M - SRC:
+        if x1 % M == 0 or x1 == NB * M - SRC:
             tok["full%d" % (x0 // M)] = list(filled)
         return fill(q, w - (x1 - x0)) if x1 - x0 < w else r
+
+    part = {}
+
+    def fill_block(q, k, w):
+        x0, l = part.get(k, (0, [t_src]))
+        c = (bs + M * k + x0) % (NB * M) if NB == 2 else M * owners[k] + x0
+        out = T.fw[:, c:c + w]
+        if q == "v":
+            r = FILL(out, 1.0)
+        elif q == "a":
+            r = COPY(out, T.fw[:, cs:cs + w], 1.0, t_src)
+        elif q == "s":
+            r = dma("s", out, T.seen[:, 0:w], "fd")
+        else:
+            r = CONST(out, [[0, w]], 1)
+        part[k] = (x0 + w, l + [r])
+        end = M - SRC * (k == NB - 1)
+        assert x0 + w <= end
+        if x0 + w == end:
+            tok["full%d" % k] = l + [r]
+            if len([j for j in range(1, NB) if "full%d" % j in tok]) == NB - 1:
+                tok["src"] = [x for j in part for x in part[j][1]]
+        return r
 
     zeros = []
 
@@ -264,29 +340,39 @@ def rank_program(g, core, T, topo):
         if q == "v":
             r = FILL(out, 0.0)
         elif q == "a":
-            r = COPY(out, T.sw[:, H * rank:H * rank + w], 0.0, *toks(*moved))
+            r = COPY(out, T.cm[:, 0:w], 1.0, tok["zero"])
         else:
             r = CONST(out, [[0, w]], 0)
         zeros.append((w, r))
+        tok["zero"] = zeros[0][1]
         if x0 + w == H:
             tok["zeros"] = [r for n, r in zeros]
         return r
 
-    t_n1 = done("p", g.iota(T.n1[:, :], [[1597, 5], [5 * 1597, 64]], -N1, 0))
-    cs = (b0 - SRC) % (4 * M)
+    lean = "Xb" in T_ORDER
+    if lean:
+        t_n1 = CONST(T.nf[:, :], [[1597, 5], [5 * 1597, 64]], 129 * M)
+        t_64 = FILL(T.f64[:, :], 64.0)
+    else:
+        t_n1 = done("p", g.iota(T.n1[:, :], [[1597, 5], [5 * 1597, 64]], -N1, 0))
     t_on = FILL(T.on[:, :], 1.0)
     t_src = FILL(T.fw[:, cs:cs + SRC], 1.0)
     filled.append(t_src)
     t_f8 = FILL(T.f8[:, :], 1.0)
     t_id = SEL(T.idt[:, :], T.on[:, :], [[-1, 128]], OP.is_equal, 0, 1, t_on)
-    t_w0 = FILL(T.c0[:, :], 0.0)
+    t_w0 = FILL(T.c0[:, 0:144 if NB == 4 else 272], 0.0)
 
-    CH = {"X": (0, 192), "Y": (192, 320)}
-    hl = {"X": T.psx[:, 0:192], "Y": T.psy[:, 0:128]}
-    cb = {"X": T.psx[:, 192:384], "Y": T.psy[:, 128:256]}
+    wx = CH["X"][1] - CH["X"][0]
+    hl = {"W": T.n2[:, 0:64], "X": T.psx[:, 0:wx], "Y": T.psy[:, 0:128]}
+    cb = {"X": T.psx[:, wx:2 * wx], "Y": T.psy[:, 128:256]}
     sdf, cf = T.cf[:, 0:1], T.cf[:, 1:2]
     pk, rp = T.psv[:, 0:256], T.psv[:, 256:512]
-    q4 = T.psr[:, 64:128]
+    q4, qo = T.psr[:, 64:128], T.psv[:, 0:64]
+    own = "W" if "W" in CH else "X"
+
+    def out_of(h, i):
+        return T["ps%d" % i][:, 256:320] if h == 0 else (T.psx, T.psy)[i % 2][:, 384:448]
+
     packed = ["p%d" % j for j in range(len(PP))]
     moved = ["e%d" % j for j in range(len(PP))]
 
@@ -294,6 +380,37 @@ def rank_program(g, core, T, topo):
         c0, c1 = CH[f]
         c = slice(c0, c1)
         cc = slice(max(c0, 64), c1)
+        lc = slice(c1 - 192, c1 - 64)
+        if f + s == "W3":
+            return TT(T.hs[:, c], T.n2[:, c], T.n2[:, c], OP.mult, tok["W1"])
+        if f + s == "W4" and not lean:
+            return TS(T.hs2[:, c], T.hs[:, c], 1.0 / M, OP.mult, cf, OP.add, tok["W3"], tok["cf"])
+        if f + s == "Ws":
+            return TT(T.sq[:, c], T.hb[:, c], T.hb[:, c], OP.mult, tok["W5"])
+        if lean:
+            if s == "0":
+                return TS(T.hx[:, c], T.nf[:, c], 64.0, OP.mult, sdf, OP.add, t_n1, tok["sdf"])
+            x0 = CH["X"][0]
+            if s == "h":
+                return ACT(T.hf[:, x0:320], T.nf[:, x0:320], AF.Identity, 64.0, sdf, t_n1, tok["sdf"])
+            if s == "w":
+                return ACT(T.hw[:, x0:320], T.hf[:, x0:320], AF.Copy, -1.0, 64 * 2047.5, tok["Xh"])
+            if s == "a":
+                need("t", [t_n1, t_64])
+                return done("t", t.matmul(hl[f], T.f64[0:1, :], T.nf[0:1, c], True, False))
+            if s == "b":
+                need("t", [t_id] + toks("Xw", f + "a"))
+                return done("t", t.matmul(hl[f], T.idt[:, :], T.hw[:, c], False, True))
+            if s == "3":
+                return ACT(T.hs[:, c], hl[f], AF.Square, 1.0, sdf, tok[f + "b"])
+            if s == "4" and "hi" not in V_ORDER:
+                return TS(T.hs2[:, c], T.hs[:, c], cf, OP.add, 1.0 / M, OP.mult, tok[f + "3"], tok["cf"])
+            if s == "4":
+                return TS(T.hs2[:, c], T.hs[:, c], 1.0 / M, OP.mult, cf, OP.add, tok[f + "3"], tok["cf"])
+            if f != "W" and s == "s":
+                return ACT(hl[f], cb[f], AF.Square, 1.0 / (2 * M), 2047.5, tok[f + "6"])
+            if f != "W" and s == "7":
+                return TT(T.ht2[:, c], hl[f], T.hf[:, c], OP.add, tok[f + "s"])
         if s == "0":
             return TS(T.hx[:, c], T.n1[:, c], sdf, OP.add, 64.0, OP.mult, t_n1, tok["sdf"])
         if s == "1":
@@ -314,42 +431,89 @@ def rank_program(g, core, T, topo):
             return TT(T.ht2[:, c], hl[f], T.sq[:, c], OP.add, tok[f + "s"])
         if s == "8":
             return TS(T.ha[:, cc], T.ht2[:, cc], 6, OP.arith_shift_right, 4095, OP.bitwise_and, tok[f + "7"])
-        i = (cc.start - 64) // 64
-        return CP(T.l1[:, c1 - 192:c1 - 64], T.off[:, c1 - 192:c1 - 64], *toks("o%d" % i, "o%d" % (i + 1)))
+        both = toks("o%d" % (lc.start // 64), "o%d" % (lc.start // 64 + 1))
+        if s == "m":
+            return TS(T.of2[:, lc], T.off[:, lc], 2 * M - 1, OP.bitwise_and, None, None, *both)
+        if "Xm" in V_ORDER:
+            return CP(T.l1[:, lc], T.of2[:, lc], tok[f + "m"])
+        return CP(T.l1[:, lc], T.off[:, lc], *both)
 
     parts = {}
     all_s = ("ah", 3 * len(HP) * ne)
     all_v = ("av", 3 * len(VP) * ne)
 
     def look(q, n):
+        if n[0] == "F" and n[1] != ":":
+            return fill_block(q, int(n[1]), int(n[3:]))
         if n[0] in "FZ":
             return (fill if n[0] == "F" else zero)(q, int(n[2:]))
         name, c0, c1 = n.split(":")
         i, c0, c1 = int(name[1]), int(c0), int(c1)
         out, win, lst, deps = {
-            "T": lambda: (T["ga%d" % i], T.fw, T.l1, [max(toks("f0", "f1", "f2", "f3")), tok["XY"[i // 2] + "l"]]),
-            "H": lambda: (T["gb%d" % i], T.sw, T.l2, [all_s] + toks("i%d" % i, *moved)),
-            "V": lambda: (T.yt, T.vw, T.l3, [all_v] + toks("l3", *["lv%d" % j for j in range(len(VP))]))}[name[0]]()
-        out, x = out[:, 16 * c0:16 * c1], win[:, :].indirect(lst[:, 64 * i + c0:64 * i + c1])
+            "T": lambda: (T["ga%d" % i], T.fw[:, 0:NB * M], T.l1, [max(toks("f0", "f1", "f2", "f3")), tok["XY"[i // 2] + "l"]]),
+            "H": lambda: (T["gb%d" % i], T.sw[:, :], T.l2, [all_s] + toks("i%d" % i, *moved)),
+            "V": lambda: (T.yt, T.vw[:, :], T.l3, [all_v] + toks("l3", *["lv%d" % j for j in range(len(VP))]))}[name[0]]()
+        out, x = out[:, 16 * c0:16 * c1], win.indirect(lst[:, 64 * i + c0:64 * i + c1])
         r = CP(out, x, *deps) if q == "v" else COPY(out, x, 1.0, *deps)
         parts[name] = parts.get(name, []) + [(c1 - c0, r)]
         if sum([w for w, r in parts[name]]) == K:
             tok["g" + name] = [r for w, r in parts[name]]
         return r
 
+    def table(q, n):
+        s, h = int(n[1]), "ab".index(n[2])
+        ps = (T.psv, T.ps3)[h]
+        x, y = ps[:, 0:128], ps[:, 128:256]
+        f = [T.ft[:, 256 * j + 128 * h:256 * j + 128 * h + 128] for j in range(3)]
+        dep = tok["k%d%s" % (s - 1, n[2])] if s else ld_t
+        if s == 0:
+            r = TS(x, T.ta[:, 128 * h:128 * h + 128], float(2 * M), OP.mult, -float(MID), OP.add, dep)
+        elif s == 1:
+            r = TT(x, x, T.ta[:, 256 + 128 * h:384 + 128 * h], OP.add, dep)
+        elif s in (2, 4):
+            r = CP(f[s // 2 - 1], (x, y)[s // 2 - 1], dep) if q == "v" else COPY(f[s // 2 - 1], (x, y)[s // 2 - 1], 1.0, dep)
+        elif s == 3:
+            r = TT(y, x, f[0], OP.subtract, dep)
+        else:
+            r = TT(f[2], y, f[1], OP.subtract, dep)
+        return r
+
+    def made_k(j):
+        return toks("k%da" % j, "k%db" % j) if "k0a" in V_ORDER else toks("k%d" % j)
+
     first, keep, rest = T.psv[:, 192:256], T.psv[:, 256:320], T.psv[:, 320:384]
+    whole = "scan" in V_ORDER
+    last = "fma" in V_ORDER
+    if last:
+        rest, keep = T.psv[:, 256:384:2], T.psv[:, 257:384:2]
+    steps = T.psv[:, 0:256]
+
+    def cand(j):
+        if j == 0 and ("z1" in V_ORDER or "z2" in P_ORDER):
+            return steps[:, 3::4]
+        if j == 2 and "z2" in P_ORDER:
+            return T.psv[:, 256:320]
+        return T.cc[:, 64 * j:64 * j + 64]
 
     def vop(n):
         j = int(n[1:]) if n[1:].isdigit() else 0
         c = slice(64 * j, 64 * j + 64)
         if ":" in n:
             return look("v", n)
-        if n[0] in "XY":
+        if n[0] in "WXY":
             return hash_step(n[0], n[1])
+        if n[0] == "k" and len(n) == 3:
+            return table("v", n)
+        if n == "lo":
+            return TS(T.col[:, 0:1], T.sdi[:, :], M - 1, OP.bitwise_and, None, None, ld_s)
+        if n == "sdf" and lean:
+            return TS(sdf, T.col[:, 0:1], 64.0, OP.mult, None, None, tok["lo"])
         if n == "sdf":
             return CP(sdf, T.sdi[:, :], ld_s)
         if n == "hi":
             return TS(T.col[:, 1:2], T.sdi[:, :], 6, OP.logical_shift_right, 64 * 4095, OP.bitwise_and, ld_s)
+        if n == "cf" and "hi" not in V_ORDER:
+            return TS(cf, T.sdi[:, :], 64.0, OP.mult, sdf, OP.subtract, tok["sdf"])
         if n == "cf":
             return CP(cf, T.col[:, 1:2], tok["hi"])
         if n == "r0":
@@ -369,36 +533,61 @@ def rank_program(g, core, T, topo):
         if n == "k5":
             return TT(T.ft[:, 512:768], rp, T.ft[:, 256:512], OP.subtract, tok["k4"])
         if n == "am":
-            return TS(T.am[:, :], T.ht2[:, 0:64], 4, OP.arith_shift_right, 12288, OP.bitwise_and, tok["X7"])
+            return TS(T.am[:, :], T.ht2[:, 0:64], 4, OP.arith_shift_right, 12288, OP.bitwise_and, tok[own + "7"])
         if n == "cw":
             return TT(T.cw[:, :], T.hb[:, 0:64], T.am[:, :], OP.add, tok["am"])
         if n[0] == "g":
             lim = T.psr[:, j:j + 1] if j < 4 else float(M * (j - 3))
             return TS(T.og[:, c], T.cw[:, :], lim, OP.is_ge, T.psr[:, 4 + j:5 + j], OP.mult, tok["cw"], tok["psr"])
+        if n in ("q0", "q1"):
+            return TS(T.pen[:, c], q4, float(2 * M), (OP.is_ge, OP.is_lt)[j], float(2 * M), OP.mult, tok["q4"])
+        if n == "qo":
+            return TT(qo, q4, T.pen[:, 0:64], OP.subtract, tok["q0"], tok["k5"])
         if n[0] == "o":
-            return TT(T.off[:, c], q4, T.ha[:, 64 * j + 64:64 * j + 128], OP.add, tok["q4"], tok["XY"[j // 2] + "8"])
+            q = "qo" if "qo" in V_ORDER else "q4"
+            return TT(T.off[:, c], qo if q == "qo" else q4, T.ha[:, 64 * j + 64:64 * j + 128], OP.add, tok[q], tok["XY"[j // 2] + "8"])
         if n == "ceX":
-            return TT(T.ce[:, 0:128], T.psx[:, 256:384], T.ha[:, 64:192], OP.add, tok["X8"])
+            return TT(T.ce[:, 0:128], T.psx[:, 2 * wx - 128:2 * wx], T.ha[:, 64:192], OP.add, tok["X8"])
         if n == "ceY":
             return TT(T.ce[:, 128:256], cb["Y"], T.ha[:, 192:320], OP.add, tok["Y8"])
-        if n[0] == "m":
-            return TT(T.xi[:, c], T["ps%d" % j][:, 256:320], T.ce[:, c], OP.min, tok["T%d" % j], tok["ce" + "XY"[j // 2]])
+        if n[0] == "m" and NB == 2:
+            return TT(T.xi[:, c], out_of(1, j), T.mt[:, c], OP.min, tok["U%d" % j], tok["M%d" % j])
+        if n[0] in "mM":
+            return TT((T.xi if n[0] == "m" else T.mt)[:, c], out_of(0, j), T.ce[:, c], OP.min, tok["T%d" % j], tok["ce" + "XY"[j // 2]])
         if n[0] == "a":
             return TS(T.ai[:, c], T.xi[:, c], M - 1, OP.bitwise_and, None, None, tok["m%d" % j])
         if n[0] == "c":
-            return TT(T.cc[:, c], q4, T.ai[:, c], OP.add, tok["a%d" % j])
+            return TT(cand(j), q4, T.ai[:, c], OP.add, tok["a%d" % j])
         if n[0] == "i":
-            return TS(T.l2[:, c], T.cc[:, c], 0.5, OP.mult, -0.25, OP.add, tok["c%d" % j])
+            return TS(T.l2[:, c], cand(j), 0.5, OP.mult, -0.25, OP.add, tok["c%d" % j])
+        if n[0] == "d" and "z2" in P_ORDER:
+            toks(("i0", "d0", "d0")[j])
+        if n in ("d0", "d1") and "z2" in P_ORDER:
+            return TT(steps[:, 2 - j::4], cand(j + 1), cand(j), OP.subtract, *toks("c%d" % j, "c%d" % (j + 1)))
+        if n == "z1":
+            tok["z0"] = FILL(T.sf[:, 0::4], 0)
+            return tok["z0"]
         if n[0] == "b":
             return TS(T.ah[:, c], T.xi[:, c], 1, OP.bitwise_and, None, None, tok["m%d" % j])
         if n[0] == "w":
             return TS(T.mh[:, c], T.ah[:, c], -15.0, OP.mult, 16.0, OP.add, tok["b%d" % j])
         if n[0] == "d":
-            return TT(T.psv[:, c], T.ai[:, 64 * j + 64:64 * j + 128], T.ai[:, c], OP.subtract, *toks("a%d" % j, "a%d" % (j + 1)))
+            out = steps[:, 2 - j::4] if whole else T.psv[:, c]
+            return TT(out, T.ai[:, 64 * j + 64:64 * j + 128], T.ai[:, c], OP.subtract, *toks("a%d" % j, "a%d" % (j + 1)))
         if n[0] == "n":
             return TT(T.vi[:, c], T["ps%d" % j][:, 384:448], T.mh[:, c], OP.mult, tok["H%d" % j], tok["w%d" % j])
+        if n == "z0":
+            if whole:
+                CP(steps[:, 3::4], T.cc[:, 0:64], tok["c0"])
+                return FILL(T.sf[:, 0::4], 0)
+            return FILL(T.sf[:, 0:128:2], 0)
+        if n == "scan":
+            return SCAN(T.so[:, :], T.sf[:, :], steps, *toks("s0", "s1", "s2", "z0", "d0", "d1", "d2", "c0"))
+        if n == "fma":
+            return SCAN(T.so[:, 0:128], T.sf[:, 0:128], T.psv[:, 256:384], *toks("s2", "z0", "keep", "rest"))
         if n[0] == "s":
-            return TS(T.vb[:, c], T.vi[:, c], 4 + rank, OP.arith_shift_right, 1, OP.bitwise_and, tok["n%d" % j])
+            out = T.sf[:, 3 - j::4] if whole else T.sf[:, 1:128:2] if last and j == 2 else T.vb[:, c]
+            return TS(out, T.vi[:, c], 4 + rank, OP.arith_shift_right, 1, OP.bitwise_and, tok["n%d" % j])
         if n == "u0":
             return TT(T.uu[:, 0:64], T.psv[:, 0:64], T.vb[:, 0:64], OP.mult, tok["s0"], tok["d0"])
         if n == "first":
@@ -413,15 +602,24 @@ def rank_program(g, core, T, topo):
             return TT(keep, first, T.uu[:, 64:128], OP.add, tok["u1"], tok["first"])
         if n == "u2":
             return TT(T.uu[:, 128:192], rest, T.vb[:, 128:192], OP.mult, tok["s2"], tok["rest"])
+        if whole or last:
+            res = T.so[:, 3::4] if whole else T.so[:, 1:128:2]
+            return CP(T.xx[:, :] if n == "x" else T.l3[:, :], res, tok["scan" if whole else "fma"])
         if n == "x":
             return TT(T.xx[:, :], keep, T.uu[:, 128:192], OP.add, tok["u2"], tok["keep"])
         return CP(T.l3[:, :], T.xx[:, :], tok["x"])
 
     def aop(n):
+        if n[0] in "fyc":
+            return sop(n, "a")
         if ":" in n:
             return look("a", n)
         if n[0] in "XY":
             return hash_step(n[0], n[1])
+        if n == "x":
+            return COPY(T.xx[:, :], T.so[:, 3::4] if whole else T.so[:, 1:128:2], 1.0, tok["scan" if whole else "fma"])
+        if n[0] == "k" and len(n) == 3:
+            return table("a", n)
         if n == "k2":
             return COPY(T.ft[:, 0:256], pk, 1.0, tok["k1"])
         if n == "k4":
@@ -435,22 +633,30 @@ def rank_program(g, core, T, topo):
         return COPY(T.sw[:, H * rank + x0:H * rank + x1], T["ps%d" % j][:, 0:x1 - x0], 1.0, tok["p%d" % j])
 
     def top(n):
+        if n[0] in "XY":
+            return hash_step(n[0], n[1])
         if n == "psr":
             return done("t", group(T.psr[:, 0:11], [(T.gs[:, :], T.rkf[:, 0:11])], *toks("r0", "r1", "gs")))
         if n == "q4":
-            return done("t", group(q4, [(T.id4k[:, :], T.og[:, 64 * j:64 * j + 64]) for j in range(7)], *toks("g6", "id4")))
+            return done("t", group(q4, [(T.id4k[:, :], T.og[:, 64 * j:64 * j + 64]) for j in range(7)],
+                                   max(toks(*["g%d" % j for j in range(7)])), tok["id4"]))
         i = int(n[1])
         ps = T["ps%d" % i]
         if n[0] == "p":
-            x0, x1 = b0 + 2 * PP[i][0], b0 + 2 * PP[i][1]
+            x0, x1 = bs + 2 * PP[i][0], bs + 2 * PP[i][1]
             ins = group(ps[:, 0:(x1 - x0) // 2], [(T.idt[:, :], T.fw[:, x0:x1:2]), (T.id16[:, :], T.fw[:, x0 + 1:x1:2])],
-                        tok[["ls%d" % j for j, (y0, y1) in enumerate(SP) if y0 <= PP[i][0] < y1][0]], t_id, tok["id16"])
+                        tok[["ls%d" % j for j, (y0, y1) in enumerate(SP) if y0 <= PP[i][0] < y1][0]], t_id, tok["id16"],
+                        *(toks("k5b") if i == 3 and "k0a" in V_ORDER else []))
         elif n[0] == "H":
             ins = group(ps[:, 384:448], [(T.cm[:, 127 * u:127 * u + 128], T["gb%d" % i][:, u::16]) for u in range(16)],
                         tok["con"], *tok["g" + n])
         else:
-            ins = group(ps[:, 256:320], [(T.c0[:, 15 - u:143 - u], T["ga%d" % i][:, u::16]) for u in range(16)],
-                        tok["wt"], *(tok["g" + n] + toks(*moved)))
+            h = "TU".index(n[0])
+            free = toks(*moved) if h == 0 else toks("ceX", "ceY") if i < 2 else toks("m%d" % (i - 2))
+            far = [(T.id4k[:, :], T.pen[:, 64 * h:64 * h + 64])] if NB == 2 else []
+            ins = group(out_of(h, i), far +
+                        [(T.c0[:, 128 * h + 15 - u:128 * h + 143 - u], T["ga%d" % i][:, u::16]) for u in range(16)],
+                        tok["wt%d" % h], *(tok["gT%d" % i] + free + (toks("q%d" % h) if far else [])))
         return done("t", ins)
 
     lr = [0]
@@ -465,37 +671,50 @@ def rank_program(g, core, T, topo):
             return look("p", n)
         if n == "gs":
             return SEL(T.gs[:, :], T.f8[:, :], [[-1, 8], [0, 16]], OP.is_equal, 0, 1, t_f8)
+        if n == "z2":
+            tok["z0"] = done("p", g.iota(T.sf[:, 0::4], [[0, 64]], 0, 0))
+            return tok["z0"]
         if n == "kc":
             CONST(T.kc[:, 0:4], [[M, 4]], 0)
             return CONST(T.kc[:, 4:8], [[-1, 4]], 0)
-        if n == "wt":
-            w = T.c0[:, 15:143:16]
-            x = SEL(w, T.on[:, 0:8], [[-16, 8]], OP.is_ge, 0, 1, t_w0)
-            return SEL(w, w, [[16, 8]], OP.is_ge, 2, -1, x)
+        if n[:2] == "wt":
+            h = int(n[2])
+            w = T.c0[:, 128 * h + 15:128 * h + 143:16]
+            x = SEL(w, T.on[:, 0:8], [[-16, 8]], OP.is_ge, -3 * h, 1, t_w0)
+            return SEL(w, w, [[16, 8]], OP.is_ge, 3 * h + 2, -1, x)
+        nh = 4 // NB
+        w = T.c0[:, 15:15 + 128 * nh:16]
+        if n == "wa":
+            return SEL(w, T.on[:, 0:8 * nh], [[-3, nh], [-16, 8]], OP.is_ge, 0, 1, t_w0)
+        if n == "wb":
+            tok["wt0"] = tok["wt1"] = SEL(w, w, [[3, nh], [16, 8]], OP.is_ge, 2, -1, tok["wa"])
+            return tok["wt0"]
         if n == "con":
             return SEL(T.cm[:, 0:2048:16], T.on[:, :], [[-1, 16], [-16, 8]], OP.is_equal, 0, 1, *tok["zeros"])
         if n == "hold":
-            return need("p", tok["full3"])
+            return need("p", [("aft%d" % T.rank_of(c), 3 * len(topo.engines(c, core))) for c in others])
+        if n[0] == "@":
+            return need("p", toks(n[1:]))
         j = int(n[1])
         out, sem, way = piece(T, rank, n)
         if n[0] == "t":
-            x, deps = T.ft[:, 256 * j:256 * j + 256], toks(("k2", "k4", "k5")[j])
+            x, deps = T.ft[:, 256 * j:256 * j + 256], made_k((2, 4, 5)[j])
         else:
             x, deps = out, toks(*["e%d" % i for i in range(len(PP)) if PP[i][2] == j]) if n[0] == "h" else toks("lv%d" % j)
         if way == "s":
-            return send(others[::-1] if n[0] == "t" else others, x, sem, out, *deps)
+            return send(others[::-1] if n[0] == "t" and not SYM else others, x, sem, out, *deps)
         if way == "n":
             return send([hc], x, n, out, *deps)
         send([helper_of(across(core, T, topo), T, topo)], x, n, out, *deps)
         return send([c for c in others if topo.die(c) == topo.die(core)], x, sem, out)
 
-    def sop(n):
+    def sop(n, dq="s"):
         if n == "chosen":
-            return dma("s", T.chosen[:, :], T.xx[:, :], "st", tok["x"])
+            return dma(dq, T.chosen[:, :], T.xx[:, :], "st", tok["x"])
         if n[0] == "y":
             c0, c1 = [int(c) for c in n.split(":")[1:]]
             deps = toks(*[m for m in V_ORDER + A_ORDER if m[:2] == "V0" and c0 <= int(m.split(":")[1]) < c1])
-            return dma("s", T.y[:, 16 * c0:16 * c1], T.yt[:, 16 * c0:16 * c1], "st", *deps)
+            return dma(dq, T.y[:, 16 * c0:16 * c1], T.yt[:, 16 * c0:16 * c1], "st", *deps)
         if n[0] == "F":
             return look("s", n)
         if n[0] == "@":
@@ -505,13 +724,15 @@ def rank_program(g, core, T, topo):
             return s_vec(k)
         if n[0] == "s":
             return s_seen(k)
-        q = (rank + k) % 4
-        if k == 0:
-            deps = toks("k2", "k4", "k5", *packed)
-        else:
-            deps = tok["full%d" % k] + [("aft%d" % q, 3 * len(topo.engines(T.cores[q], core)))]
+        q = owners[k]
+        deps = made_k(2) + made_k(4) + made_k(5) if k == 0 else [("aft%d" % q, 3 * len(topo.engines(T.cores[q], core)))]
+        blk = (q % NB - bs // M) % NB if NB == 2 else k
+        deps += tok["full%d" % blk] if blk else toks(*packed)
+        if part and blk == NB - 1:
+            deps += tok["src"]
         for f in range(3):
-            x = dma("s", T.fw[f::16, M * q:M * q + M], T.ft[:, 256 * f:256 * f + 256] if k == 0 else T.fl[3 * q + f], "fx", *deps)
+            x = dma(dq, T.fw[3 * (q // NB) + f::16, M * (q % NB):M * (q % NB) + M],
+                    T.ft[:, 256 * f:256 * f + 256] if k == 0 else T.fl[3 * q + f], "fx", *deps)
         return x
 
     queues = [(list(V_ORDER), vop), (list(A_ORDER), aop), (list(T_ORDER), top), (list(P_ORDER), pop), (list(S_ORDER), sop)]

from concourse.bass import DstId, RemoteDMATransfer
from concourse.mybir import AluOpType as OP, ActivationFunctionType as AF

M, K = 4096, 64
H = M // 2
MID = 1 << 24
N1 = 1 << 23
NB = 4
SYM = 0
CH = {"X": (0, 192), "Y": (192, 320)}
TP = ["s", "s", "s"]
HP = [(0, 512, "n"), (512, 1536, "n"), (1536, 2048, "n")]
VP = [(0, 256, "n"), (256, 1920, "n"), (1920, 4096, "s")]
HELPER_ORDER = "v0 h0 h1 h2 v1".split()
SP = [(0, 1024), (1024, 2048)]
PP = [(0, 512, 0), (512, 1024, 1), (1024, 1536, 1), (1536, 2048, 2)]
SRC = 1024
LOADS = "d t v0 s0 r s1".split()
P_ORDER = "kc v0 F:256 t0 gs t1 t2 h0 F:1024 h1 h2 Z:768 wt0 v1 v2 Z:768 con".split()
S_ORDER = "f0 f1 f2 f3 v1 v2 chosen y:0:18 y:34:50 y:18:34 y:50:64".split()
A_ORDER = ("F:768 id16 F:1024 id4 F:768 X3 Y3 e0 e1 F:512 Xs Ys e2 e3 F:256 F:1024 "
           "T0:0:30 T1:0:32 T2:0:40 T3:0:48 H0:0:40 H1:0:48 H2:0:40 V0:34:50 V0:50:64").split()
V_ORDER = ("F:1024 F:1024 sdf hi k0 X0 cf k1 X1 Y0 k2 Y1 X2 k3 r0 Y2 k4 k5 X4 Y4 X5 r1 Y5 X6 Y6 F:768 F:1024 X7 Y7 am cw "
           "F:1024 g0 Y8 g1 X8 g2 g3 g4 g5 F:768 g6 ceX Z:512 o0 o1 ceY o2 o3 Xl Yl "
           "T0:30:64 T1:32:64 T2:48:64 m0 T2:40:48 a0 b0 c0 m1 T3:56:64 i0 b1 a1 T3:48:56 w0 c1 d0 w1 i1 m2 H0:40:64 a2 b2 "
           "c2 w2 d1 m3 i2 H1:48:64 a3 n0 d2 s0 z0 H2:40:64 n1 s1 n2 s2 scan l3 x V0:0:18 V0:18:34").split()
T_ORDER = "p0 p1 p2 p3 psr q4 T0 T1 T2 T3 H0 H1 H2".split()
CH = {"W": (0, 64), "X": (64, 192), "Y": (192, 320)}
P_ORDER = 'kc gs v0 t0 wa t1 wb t2 h0 F2:512 h1 h2 F3:512 Z:768 v1 v2 Z:768 con'.split()
S_ORDER = 'f0 f1 f2 f3 v1 v2 chosen y:0:34 y:34:64'.split()
A_ORDER = 'F1:1024 id16 F2:512 F1:768 F2:512 id4 F2:512 e0 e1 Y3 F1:256 X3 e2 e3 F3:768 Xs Ys T0:0:32 T1:0:34 T2:0:34 T3:0:44 H0:0:46 H1:0:42 H2:0:30 x V0:18:34 V0:50:64'.split()
V_ORDER = 'F1:1024 F1:1024 sdf hi k0 W0 X0 Y0 W1 k1 X1 cf W3 k2 r0 W4 Y1 k3 X2 W5 k4 Ws Y2 k5 W7 F2:1024 r1 am F2:1024 X4 cw Y4 X5 g3 g2 Y5 F3:768 X6 Y6 F3:1024 g6 g1 g0 X7 g5 g4 Y7 X8 Z:512 Y8 o1 o0 o2 o3 Xl ceX Yl T0:32:64 T1:34:64 T2:34:54 ceY m0 T2:54:64 a0 b0 m1 c0 T3:58:64 a1 i0 T3:44:58 m2 c1 b1 a2 i1 H0:46:64 c2 b2 z0 i2 H1:42:64 H2:30:64 m3 w1 w0 d0 a3 w2 n0 d1 n1 d2 n2 s1 s0 s2 scan l3 V0:0:18 V0:34:50'.split()
T_ORDER = 'p0 p1 p2 p3 psr q4 T0 T1 T2 T3 H0 H1 H2'.split()
CH = {"X": (0, 192), "Y": (192, 320)}
P_ORDER = 'kc gs v0 t0 wa t1 wb t2 h0 F3:512 h1 h2 Z:1024 Z:512 con v1 v2'.split()
S_ORDER = 'F1:2048 f0 f1 f2 f3 @T0:34:64 v1 v2 chosen y:0:34 y:34:64'.split()
A_ORDER = 'F1:512 id16 Xh Xw k2 X3 F3:512 k4 e0 Y3 F2:512 Xs e1 e2 e3 Ys id4 T0:0:34 T1:0:26 T2:0:38 T3:0:44 H0:0:42 H1:0:36 H2:0:32 x V0:18:34 V0:50:64'.split()
V_ORDER = 'F2:512 lo F2:512 sdf F2:512 k0 F1:512 k1 F2:512 F3:512 r0 cf k3 F1:512 X4 r1 F2:512 X5 k5 X6 F2:512 F3:512 Y4 F1:512 F3:512 X7 F2:512 am F3:512 X8 Y5 z1 cw Y6 g3 g6 g2 g1 g4 g0 g5 ceX Y7 Z:512 Y8 o0 o1 o2 o3 Xl Yl ceY T0:34:64 T1:26:64 T2:38:56 m0 T2:56:64 a0 T3:44:58 c0 m1 T3:58:64 i0 a1 b0 m2 b1 c1 a2 b2 i1 c2 H0:42:64 i2 H1:36:64 H2:32:64 m3 w0 d0 w1 d1 a3 n1 n0 w2 d2 s0 n2 s1 s2 scan l3 V0:0:18 V0:34:50'.split()
T_ORDER = 'Xa Ya Xb Yb p0 p1 psr p2 p3 q4 T0 T1 T2 T3 H0 H1 H2'.split()
SYM = 1
HP = [(0, 1024, "n"), (1024, 2048, "n")]
PP = [(0, 512, 0), (512, 1024, 0), (1024, 1536, 1), (1536, 2048, 1)]
VP = [(0, 256, 'n'), (256, 832, 'n'), (832, 2496, 'n'), (2496, 4096, 's')]
HELPER_ORDER = 'v0 v1 h0 h1 v2'.split()
P_ORDER = 'gs kc v0 wa t0 t1 v1 t2 h0 F3:512 wb h1 Z:1024 v2 v3 Z:512 con'.split()
S_ORDER = 'v1 f0 f1 f2 f3 v2 v3 chosen y:0:34 y:34:64'.split()
A_ORDER = 'F2:512 F1:512 id16 Xh Xw k2 F2:512 X3 k4 e0 F2:512 e1 Xs Y3 e2 F3:512 e3 Ys id4 T0:0:22 T1:0:34 T2:0:42 T3:0:60 H0:0:42 H1:0:24 H2:0:38 x V0:18:34 V0:50:64'.split()
V_ORDER = 'F2:512 lo F2:512 sdf k0 F3:512 k1 F1:512 F1:512 F2:512 F1:512 k3 F1:512 cf F1:512 F1:512 F3:512 X4 r0 k5 X5 r1 X6 F2:512 F2:512 F3:512 Y4 X7 F1:512 X8 Y5 am ceX F3:512 cw Y6 g6 g0 g2 g4 g1 g3 g5 z1 Y7 Z:512 Y8 o0 o1 o3 Xl o2 ceY Yl T0:22:64 T1:34:64 T2:46:64 m0 T2:42:46 a0 b0 T3:60:62 m1 c0 T3:62:64 b1 a1 i0 w1 m2 w0 c1 a2 b2 i1 c2 H0:42:64 i2 H1:24:64 m3 H2:38:64 w2 n0 n1 a3 d0 s1 d2 s0 n2 d1 s2 scan l3 V0:0:18 V0:34:50'.split()
T_ORDER = 'Xa Xb p0 p1 p2 Ya Yb psr p3 q4 T0 T1 T2 T3 H0 H1 H2'.split()
P_ORDER = 'gs z2 v0 t0 kc t1 v1 wa t2 h0 F2:512 h1 wb Z:512 Z:1024 v2 v3 Z:512 con'.split()
S_ORDER = 'v1 f0 f2 f1 f3 v2 v3 chosen y:0:34 y:34:64'.split()
A_ORDER = 'F1:512 F3:512 Xh id16 Xw F1:512 X3 k4 Y3 e0 e1 Xs e2 e3 F3:512 F3:512 id4 Ys T0:0:30 T1:0:40 T2:0:28 T3:0:50 H0:0:46 H1:0:36 H2:0:30 x V0:18:34 V0:50:64'.split()
V_ORDER = 'F2:512 lo F2:512 sdf k0 F2:512 k1 F1:512 k2 cf F3:512 k3 F2:512 F1:512 F2:512 X4 k5 X5 F3:512 X6 F1:512 F2:512 r0 F1:512 X7 Y4 F2:512 F3:512 am r1 Y5 F1:512 cw F1:512 g3 Y6 g5 g2 g0 g1 g4 g6 Y7 X8 Y8 o1 o0 o2 o3 Xl ceX Yl ceY T0:30:64 T1:40:64 T2:28:58 m0 T2:58:64 a0 T3:50:60 c0 b0 m1 i0 T3:60:64 a1 m2 b1 c1 a2 w0 i1 d0 c2 H0:46:64 i2 H1:36:64 H2:30:64 m3 n0 b2 a3 w1 s0 w2 d2 n1 n2 d1 s1 s2 scan l3 V0:0:18 V0:34:50'.split()
T_ORDER = 'Xa Ya Xb Yb p0 p1 p2 p3 psr q4 T0 T1 T2 T3 H0 H1 H2'.split()
VP = [(0, 256, 'n'), (256, 704, 'n'), (704, 2112, 'n'), (2112, 4096, 's')]
SCRATCH = {
    "fw": ("sbuf", [128, 4 * M], "bfloat16"),
    "sw": ("sbuf", [128, 4 * H], "bfloat16"),
    "vw": ("sbuf", [128, 4 * M], "bfloat16"),
    "fl": ("dram", [12, 128, 256], "bfloat16"),
    "ta": ("sbuf", [128, 512], "int32"),
    "ft": ("sbuf", [128, 768], "bfloat16"),
    "sdi": ("sbuf", [128, 1], "int32"),
    "col": ("sbuf", [128, 2], "int32"),
    "cf": ("sbuf", [128, 4], "float32"),
    "rki": ("sbuf", [8, 8], "int32"),
    "kc": ("sbuf", [8, 8], "float32"),
    "rkf": ("sbuf", [8, 12], "float32"),
    "f8": ("sbuf", [8, 128], "float32"),
    "gs": ("sbuf", [8, 128], "float32"),
    "am": ("sbuf", [128, 64], "int32"),
    "cw": ("sbuf", [128, 64], "float32"),
    "og": ("sbuf", [128, 448], "bfloat16"),
    "idt": ("sbuf", [128, 128], "bfloat16"),
    "id4k": ("sbuf", [128, 128], "bfloat16"),
    "id16": ("sbuf", [128, 128], "bfloat16"),
    "cm": ("sbuf", [128, 2048], "bfloat16"),
    "c0": ("sbuf", [128, 272], "bfloat16"),
    "pen": ("sbuf", [128, 128], "bfloat16"),
    "mt": ("sbuf", [128, 256], "float32"),
    "n1": ("sbuf", [128, 320], "int32"),
    "nf": ("sbuf", [128, 320], "float32"),
    "hf": ("sbuf", [128, 320], "float32"),
    "hw": ("sbuf", [128, 320], "bfloat16"),
    "f64": ("sbuf", [1, 128], "float32"),
    "n2": ("sbuf", [128, 320], "int32"),
    "hx": ("sbuf", [128, 320], "int32"),
    "hs": ("sbuf", [128, 320], "float32"),
    "hs2": ("sbuf", [128, 320], "int32"),
    "hb": ("sbuf", [128, 320], "int32"),
    "sq": ("sbuf", [128, 320], "float32"),
    "ht2": ("sbuf", [128, 320], "int32"),
    "ha": ("sbuf", [128, 320], "int32"),
    "ce": ("sbuf", [128, 256], "float32"),
    "off": ("sbuf", [128, 256], "int32"),
    "of2": ("sbuf", [128, 256], "int32"),
    "l1": ("sbuf", [128, 256], "uint16"),
    "l2": ("sbuf", [128, 192], "uint16"),
    "l3": ("sbuf", [128, 64], "uint16"),
    "xi": ("sbuf", [128, 256], "int32"),
    "ah": ("sbuf", [128, 192], "int32"),
    "ai": ("sbuf", [128, 256], "int32"),
    "mh": ("sbuf", [128, 192], "float32"),
    "cc": ("sbuf", [128, 192], "float32"),
    "vi": ("sbuf", [128, 192], "int32"),
    "vb": ("sbuf", [128, 192], "int32"),
    "uu": ("sbuf", [128, 256], "float32"),
    "sf": ("sbuf", [128, 256], "int32"),
    "so": ("sbuf", [128, 256], "float32"),
    "xx": ("sbuf", [128, 64], "float32"),
    "yt": ("sbuf", [128, 1024], "bfloat16"),
    "on": ("sbuf", [128, 128], "bfloat16"),
    "psr": ("psum", [128, 512], "float32"),
    "psv": ("psum", [128, 512], "float32"),
    "psx": ("psum", [128, 512], "float32"),
    "psy": ("psum", [128, 512], "float32"),
}
for _i in range(4):
    SCRATCH["ga%d" % _i] = ("sbuf", [128, 1024], "bfloat16")
    SCRATCH["ps%d" % _i] = ("psum", [128, 512], "float32")
for _i in range(3):
    SCRATCH["gb%d" % _i] = ("sbuf", [128, 1024], "bfloat16")

SEMAPHORES = ["v", "a", "p", "t", "ldt", "lds", "ldr", "fd", "fx", "st", "lr", "aft0", "aft1", "aft2", "aft3", "ah", "av"]
SEMAPHORES += ["%s%d" % (s, j) for s in ("sn", "t", "h", "vc", "v") for j in range(6)]


def helper_of(core, T, topo):
    free = [c for c in topo.cores_of(core) if T.rank_of(c) is None and topo.die(c) == topo.die(core)]
    mine = [c for c in T.cores if topo.chip(c) == topo.chip(core) and topo.die(c) == topo.die(core)]
    return free[mine.index(core)]


def spread(g, T, topo, core, dsts, src, name, dst_ap):
    ids = []
    for d in dsts:
        rid, pid, _s = topo.addr(d)
        ids.append(DstId(rid=rid, pnc=pid))
    mask = topo.mask(core, dsts[0])
    for d in dsts:
        mask &= topo.mask(core, d)
    g.remote_dma_fused([RemoteDMATransfer(dst_ids=ids, dma_engine_mask=mask, remote_sem=T.sem[name],
                                          srcs=[src], dsts=[dst_ap for d in dsts], alu_op=0)], local_sem=T.sem.lr)
    return len(topo.engines(core, dsts[0]))


def after(T, r):
    return [T.cores[(r + k) % len(T.cores)] for k in range(1, len(T.cores))]


def across(core, T, topo):
    mine = [c for c in T.cores if topo.die(c) == topo.die(core)]
    return [c for c in T.cores if c not in mine][mine.index(core)]


def turn(core, T, topo):
    if not SYM:
        return after(T, T.rank_of(core))
    a = across(core, T, topo)
    far = [a] + [c for c in T.cores if topo.die(c) == topo.die(a) and c != a]
    near = [c for c in T.cores if topo.die(c) == topo.die(core) and c != core]
    return far + near if SYM == 1 else near + far


def piece(T, r, n):
    if n[0] == "t":
        return T.fl[3 * r + int(n[1])], "aft%d" % r, TP[int(n[1])]
    x0, x1, way = (HP if n[0] == "h" else VP)[int(n[1])]
    b = (H if n[0] == "h" else M) * r
    return (T.sw if n[0] == "h" else T.vw)[:, b + x0:b + x1], "a" + n[0], way


def helper_program(g, core, T, topo, near):
    far = across(near, T, topo)
    n = 0
    for name in HELPER_ORDER:
        way = piece(T, 0, name)[2]
        if way == "n":
            owner, dsts = near, turn(near, T, topo)
        else:
            owner, dsts = far, [c for c in after(T, T.rank_of(far)) if topo.die(c) == topo.die(core)]
        x, sem, way = piece(T, T.rank_of(owner), name)
        g.wait_ge(T.sem[name], len(topo.engines(owner, core)))
        n += spread(g, T, topo, core, dsts, x, sem, x)
    g.wait_ge(T.sem.lr, n)


def rank_program(g, core, T, topo):
    rank = T.rank_of(core)
    if rank is None:
        for c in T.cores:
            if c in topo.cores_of(core) and helper_of(c, T, topo) == core:
                helper_program(g, core, T, topo, c)
        return

    others = turn(core, T, topo)
    owners = [rank] + [T.rank_of(c) for c in others]
    hc = helper_of(core, T, topo)
    ne = len(topo.engines(core, hc))
    b0 = M * rank
    bs = b0 if NB == 4 else M * (1 - rank % 2)
    cs = (bs - SRC) % (NB * M) if NB == 2 else M * owners[3] + M - SRC
    engs = {"v": g.vector, "a": g.scalar, "p": g, "t": g.tensor, "s": g.sync}
    cnt = {}
    seen = {k: {} for k in engs}
    tok = {}

    def need(q, toks):
        for name, val in toks:
            if seen[q].get(name, 0) < val:
                engs[q].wait_ge(T.sem[name], val)
                seen[q][name] = val

    def done(q, ins, n=1, sem=None):
        s = sem or q
        ins.then_inc(T.sem[s], n)
        cnt[s] = cnt.get(s, 0) + n
        return (s, cnt[s])

    def toks(*names):
        return [tok[n] for n in names]

    v, a, t = g.vector, g.scalar, g.tensor

    def TT(out, x, y, op, *deps):
        need("v", deps)
        return done("v", v.tensor_tensor(out, x, y, op))

    def TS(out, x, s1, op0, s2, op1, *deps):
        need("v", deps)
        if op1 is None:
            return done("v", v.tensor_scalar(out, x, s1, None, op0))
        return done("v", v.tensor_scalar(out, x, s1, s2, op0, op1))

    def CP(out, x, *deps):
        need("v", deps)
        return done("v", v.tensor_copy(out, x))

    def SCAN(out, x, y, *deps):
        need("v", deps)
        return done("v", v.tensor_tensor_scan(out, x, y, 0.0, OP.mult, OP.add))

    def FILL(ap, c):
        return done("v", v.memset(ap, c))

    def COPY(out, x, scale, *deps):
        need("a", deps)
        return done("a", a.activation(out, x, AF.Copy, scale=scale))

    def ACT(out, x, func, scale, bias, *deps):
        need("a", deps)
        return done("a", a.activation(out, x, func, bias=bias, scale=scale))

    def SEL(out, x, pattern, op, base, ch, *deps):
        need("p", deps)
        return done("p", g.affine_select(out, x, pattern, op, 0.0, base, ch))

    def CONST(out, pattern, c):
        return done("p", g.iota(out, pattern, c, 0, allow_small_or_imprecise_dtypes=True))

    def dma(q, out, x, sem, *deps):
        need(q, deps)
        return done(q, engs[q].dma_start(out, x), 16, sem)

    def group(out, pairs, *deps):
        need("t", deps)
        for j, (w, x) in enumerate(pairs):
            ins = t.matmul(out, w, x, j == 0, j == len(pairs) - 1)
        return ins

    def s_vec(j):
        x0, x1, way = VP[j]
        tok["lv%d" % j] = dma("s", T.vw[:, b0 + x0:b0 + x1], T.vec[:, x0:x1], "vc%d" % j)

    def s_seen(j):
        x0, x1 = SP[j]
        tok["ls%d" % j] = dma("s", T.fw[:, bs + 2 * x0:bs + 2 * x1], T.seen[:, 2 * x0:2 * x1], "sn%d" % j)

    for n in LOADS:
        if n[0] == "v":
            s_vec(int(n[1]))
        elif n == "d":
            ld_s = dma("a", T.sdi[:, :], T.sd[:, :], "lds")
        elif n == "t":
            dma("s", T.ta[:, 256:512], T.ali[:, :], "ldt")
            ld_t = dma("a", T.ta[:, 0:256], T.thr[:, :], "ldt")
        elif n == "r":
            ld_r = dma("s", T.rki[:, :], T.rk[:, :], "ldr")
        else:
            s_seen(int(n[1]))

    filled = []
    upto = [M]

    def fill(q, w):
        x0 = upto[0]
        x1 = min(x0 + w, (x0 // M + 1) * M)
        upto[0] = x1
        c = (bs + x0) % (NB * M)
        out = T.fw[:, c:c + x1 - x0]
        if q == "v":
            r = FILL(out, 1.0)
        elif q == "a":
            r = COPY(out, T.fw[:, cs:cs + x1 - x0], 1.0, t_src)
        else:
            r = CONST(out, [[0, x1 - x0]], 1)
        filled.append(r)
        if x1 % M == 0 or x1 == NB * M - SRC:
            tok["full%d" % (x0 // M)] = list(filled)
        return fill(q, w - (x1 - x0)) if x1 - x0 < w else r

    part = {}

    def fill_block(q, k, w):
        x0, l = part.get(k, (0, [t_src]))
        c = (bs + M * k + x0) % (NB * M) if NB == 2 else M * owners[k] + x0
        out = T.fw[:, c:c + w]
        if q == "v":
            r = FILL(out, 1.0)
        elif q == "a":
            r = COPY(out, T.fw[:, cs:cs + w], 1.0, t_src)
        elif q == "s":
            r = dma("s", out, T.seen[:, 0:w], "fd")
        else:
            r = CONST(out, [[0, w]], 1)
        part[k] = (x0 + w, l + [r])
        end = M - SRC * (k == NB - 1)
        assert x0 + w <= end
        if x0 + w == end:
            tok["full%d" % k] = l + [r]
            if len([j for j in range(1, NB) if "full%d" % j in tok]) == NB - 1:
                tok["src"] = [x for j in part for x in part[j][1]]
        return r

    zeros = []

    def zero(q, w):
        x0 = sum([n for n, r in zeros])
        out = T.cm[:, x0:x0 + w]
        if q == "v":
            r = FILL(out, 0.0)
        elif q == "a":
            r = COPY(out, T.cm[:, 0:w], 1.0, tok["zero"])
        else:
            r = CONST(out, [[0, w]], 0)
        zeros.append((w, r))
        tok["zero"] = zeros[0][1]
        if x0 + w == H:
            tok["zeros"] = [r for n, r in zeros]
        return r

    lean = "Xb" in T_ORDER
    if lean:
        t_n1 = CONST(T.nf[:, :], [[1597, 5], [5 * 1597, 64]], 129 * M)
        t_64 = FILL(T.f64[:, :], 64.0)
    else:
        t_n1 = done("p", g.iota(T.n1[:, :], [[1597, 5], [5 * 1597, 64]], -N1, 0))
    t_on = FILL(T.on[:, :], 1.0)
    t_src = FILL(T.fw[:, cs:cs + SRC], 1.0)
    filled.append(t_src)
    t_f8 = FILL(T.f8[:, :], 1.0)
    t_id = SEL(T.idt[:, :], T.on[:, :], [[-1, 128]], OP.is_equal, 0, 1, t_on)
    t_w0 = FILL(T.c0[:, 0:144 if NB == 4 else 272], 0.0)

    wx = CH["X"][1] - CH["X"][0]
    hl = {"W": T.n2[:, 0:64], "X": T.psx[:, 0:wx], "Y": T.psy[:, 0:128]}
    cb = {"X": T.psx[:, wx:2 * wx], "Y": T.psy[:, 128:256]}
    sdf, cf = T.cf[:, 0:1], T.cf[:, 1:2]
    pk, rp = T.psv[:, 0:256], T.psv[:, 256:512]
    q4, qo = T.psr[:, 64:128], T.psv[:, 0:64]
    own = "W" if "W" in CH else "X"

    def out_of(h, i):
        return T["ps%d" % i][:, 256:320] if h == 0 else (T.psx, T.psy)[i % 2][:, 384:448]

    packed = ["p%d" % j for j in range(len(PP))]
    moved = ["e%d" % j for j in range(len(PP))]

    def hash_step(f, s):
        c0, c1 = CH[f]
        c = slice(c0, c1)
        cc = slice(max(c0, 64), c1)
        lc = slice(c1 - 192, c1 - 64)
        if f + s == "W3":
            return TT(T.hs[:, c], T.n2[:, c], T.n2[:, c], OP.mult, tok["W1"])
        if f + s == "W4" and not lean:
            return TS(T.hs2[:, c], T.hs[:, c], 1.0 / M, OP.mult, cf, OP.add, tok["W3"], tok["cf"])
        if f + s == "Ws":
            return TT(T.sq[:, c], T.hb[:, c], T.hb[:, c], OP.mult, tok["W5"])
        if lean:
            if s == "0":
                return TS(T.hx[:, c], T.nf[:, c], 64.0, OP.mult, sdf, OP.add, t_n1, tok["sdf"])
            x0 = CH["X"][0]
            if s == "h":
                return ACT(T.hf[:, x0:320], T.nf[:, x0:320], AF.Identity, 64.0, sdf, t_n1, tok["sdf"])
            if s == "w":
                return ACT(T.hw[:, x0:320], T.hf[:, x0:320], AF.Copy, -1.0, 64 * 2047.5, tok["Xh"])
            if s == "a":
                need("t", [t_n1, t_64])
                return done("t", t.matmul(hl[f], T.f64[0:1, :], T.nf[0:1, c], True, False))
            if s == "b":
                need("t", [t_id] + toks("Xw", f + "a"))
                return done("t", t.matmul(hl[f], T.idt[:, :], T.hw[:, c], False, True))
            if s == "3":
                return ACT(T.hs[:, c], hl[f], AF.Square, 1.0, sdf, tok[f + "b"])
            if s == "4" and "hi" not in V_ORDER:
                return TS(T.hs2[:, c], T.hs[:, c], cf, OP.add, 1.0 / M, OP.mult, tok[f + "3"], tok["cf"])
            if s == "4":
                return TS(T.hs2[:, c], T.hs[:, c], 1.0 / M, OP.mult, cf, OP.add, tok[f + "3"], tok["cf"])
            if f != "W" and s == "s":
                return ACT(hl[f], cb[f], AF.Square, 1.0 / (2 * M), 2047.5, tok[f + "6"])
            if f != "W" and s == "7":
                return TT(T.ht2[:, c], hl[f], T.hf[:, c], OP.add, tok[f + "s"])
        if s == "0":
            return TS(T.hx[:, c], T.n1[:, c], sdf, OP.add, 64.0, OP.mult, t_n1, tok["sdf"])
        if s == "1":
            return TS(T.n2[:, c], T.hx[:, c], 64 * 4095, OP.bitwise_and, None, None, tok[f + "0"])
        if s == "2":
            return CP(hl[f], T.n2[:, c], tok[f + "1"])
        if s == "3":
            return ACT(T.hs[:, c], hl[f], AF.Square, 1.0 / 64, 0.0, tok[f + "2"])
        if s == "4":
            return TS(T.hs2[:, c], T.hs[:, c], cf, OP.add, None, None, tok[f + "3"], tok["cf"])
        if s == "5":
            return TS(T.hb[:, c], T.hs2[:, c], 6, OP.arith_shift_right, 4095, OP.bitwise_and, tok[f + "4"])
        if s == "6":
            return TS(cb[f], T.hb[:, c], float(2 * M), OP.mult, float(M - MID), OP.add, tok[f + "5"])
        if s == "s":
            return ACT(T.sq[:, c], cb[f], AF.Square, 1.0 / (2 * M), 2047.5, tok[f + "6"])
        if s == "7":
            return TT(T.ht2[:, c], hl[f], T.sq[:, c], OP.add, tok[f + "s"])
        if s == "8":
            return TS(T.ha[:, cc], T.ht2[:, cc], 6, OP.arith_shift_right, 4095, OP.bitwise_and, tok[f + "7"])
        both = toks("o%d" % (lc.start // 64), "o%d" % (lc.start // 64 + 1))
        if s == "m":
            return TS(T.of2[:, lc], T.off[:, lc], 2 * M - 1, OP.bitwise_and, None, None, *both)
        if "Xm" in V_ORDER:
            return CP(T.l1[:, lc], T.of2[:, lc], tok[f + "m"])
        return CP(T.l1[:, lc], T.off[:, lc], *both)

    parts = {}
    all_s = ("ah", 3 * len(HP) * ne)
    all_v = ("av", 3 * len(VP) * ne)

    def look(q, n):
        if n[0] == "F" and n[1] != ":":
            return fill_block(q, int(n[1]), int(n[3:]))
        if n[0] in "FZ":
            return (fill if n[0] == "F" else zero)(q, int(n[2:]))
        name, c0, c1 = n.split(":")
        i, c0, c1 = int(name[1]), int(c0), int(c1)
        out, win, lst, deps = {
            "T": lambda: (T["ga%d" % i], T.fw[:, 0:NB * M], T.l1, [max(toks("f0", "f1", "f2", "f3")), tok["XY"[i // 2] + "l"]]),
            "H": lambda: (T["gb%d" % i], T.sw[:, :], T.l2, [all_s] + toks("i%d" % i, *moved)),
            "V": lambda: (T.yt, T.vw[:, :], T.l3, [all_v] + toks("l3", *["lv%d" % j for j in range(len(VP))]))}[name[0]]()
        out, x = out[:, 16 * c0:16 * c1], win.indirect(lst[:, 64 * i + c0:64 * i + c1])
        r = CP(out, x, *deps) if q == "v" else COPY(out, x, 1.0, *deps)
        parts[name] = parts.get(name, []) + [(c1 - c0, r)]
        if sum([w for w, r in parts[name]]) == K:
            tok["g" + name] = [r for w, r in parts[name]]
        return r

    def table(q, n):
        s, h = int(n[1]), "ab".index(n[2])
        ps = (T.psv, T.ps3)[h]
        x, y = ps[:, 0:128], ps[:, 128:256]
        f = [T.ft[:, 256 * j + 128 * h:256 * j + 128 * h + 128] for j in range(3)]
        dep = tok["k%d%s" % (s - 1, n[2])] if s else ld_t
        if s == 0:
            r = TS(x, T.ta[:, 128 * h:128 * h + 128], float(2 * M), OP.mult, -float(MID), OP.add, dep)
        elif s == 1:
            r = TT(x, x, T.ta[:, 256 + 128 * h:384 + 128 * h], OP.add, dep)
        elif s in (2, 4):
            r = CP(f[s // 2 - 1], (x, y)[s // 2 - 1], dep) if q == "v" else COPY(f[s // 2 - 1], (x, y)[s // 2 - 1], 1.0, dep)
        elif s == 3:
            r = TT(y, x, f[0], OP.subtract, dep)
        else:
            r = TT(f[2], y, f[1], OP.subtract, dep)
        return r

    def made_k(j):
        return toks("k%da" % j, "k%db" % j) if "k0a" in V_ORDER else toks("k%d" % j)

    first, keep, rest = T.psv[:, 192:256], T.psv[:, 256:320], T.psv[:, 320:384]
    whole = "scan" in V_ORDER
    last = "fma" in V_ORDER
    if last:
        rest, keep = T.psv[:, 256:384:2], T.psv[:, 257:384:2]
    steps = T.psv[:, 0:256]

    def cand(j):
        if j == 0 and ("z1" in V_ORDER or "z2" in P_ORDER):
            return steps[:, 3::4]
        if j == 2 and "z2" in P_ORDER:
            return T.psv[:, 256:320]
        return T.cc[:, 64 * j:64 * j + 64]

    def vop(n):
        j = int(n[1:]) if n[1:].isdigit() else 0
        c = slice(64 * j, 64 * j + 64)
        if ":" in n:
            return look("v", n)
        if n[0] in "WXY":
            return hash_step(n[0], n[1])
        if n[0] == "k" and len(n) == 3:
            return table("v", n)
        if n == "lo":
            return TS(T.col[:, 0:1], T.sdi[:, :], M - 1, OP.bitwise_and, None, None, ld_s)
        if n == "sdf" and lean:
            return TS(sdf, T.col[:, 0:1], 64.0, OP.mult, None, None, tok["lo"])
        if n == "sdf":
            return CP(sdf, T.sdi[:, :], ld_s)
        if n == "hi":
            return TS(T.col[:, 1:2], T.sdi[:, :], 6, OP.logical_shift_right, 64 * 4095, OP.bitwise_and, ld_s)
        if n == "cf" and "hi" not in V_ORDER:
            return TS(cf, T.sdi[:, :], 64.0, OP.mult, sdf, OP.subtract, tok["sdf"])
        if n == "cf":
            return CP(cf, T.col[:, 1:2], tok["hi"])
        if n == "r0":
            return TT(T.rkf[:, 0:8], T.rki[:, :], T.kc[:, 0:8], OP.add, ld_r, tok["kc"])
        if n == "r1":
            return TS(T.rkf[:, 8:11], T.rkf[:, 4:7], -1.0, OP.mult, 1.0, OP.add, tok["r0"])
        if n == "k0":
            return TS(pk, T.ta[:, 0:256], float(2 * M), OP.mult, -float(MID), OP.add, ld_t)
        if n == "k1":
            return TT(pk, pk, T.ta[:, 256:512], OP.add, tok["k0"])
        if n == "k2":
            return CP(T.ft[:, 0:256], pk, tok["k1"])
        if n == "k3":
            return TT(rp, pk, T.ft[:, 0:256], OP.subtract, tok["k2"])
        if n == "k4":
            return CP(T.ft[:, 256:512], rp, tok["k3"])
        if n == "k5":
            return TT(T.ft[:, 512:768], rp, T.ft[:, 256:512], OP.subtract, tok["k4"])
        if n == "am":
            return TS(T.am[:, :], T.ht2[:, 0:64], 4, OP.arith_shift_right, 12288, OP.bitwise_and, tok[own + "7"])
        if n == "cw":
            return TT(T.cw[:, :], T.hb[:, 0:64], T.am[:, :], OP.add, tok["am"])
        if n[0] == "g":
            lim = T.psr[:, j:j + 1] if j < 4 else float(M * (j - 3))
            return TS(T.og[:, c], T.cw[:, :], lim, OP.is_ge, T.psr[:, 4 + j:5 + j], OP.mult, tok["cw"], tok["psr"])
        if n in ("q0", "q1"):
            return TS(T.pen[:, c], q4, float(2 * M), (OP.is_ge, OP.is_lt)[j], float(2 * M), OP.mult, tok["q4"])
        if n == "qo":
            return TT(qo, q4, T.pen[:, 0:64], OP.subtract, tok["q0"], tok["k5"])
        if n[0] == "o":
            q = "qo" if "qo" in V_ORDER else "q4"
            return TT(T.off[:, c], qo if q == "qo" else q4, T.ha[:, 64 * j + 64:64 * j + 128], OP.add, tok[q], tok["XY"[j // 2] + "8"])
        if n == "ceX":
            return TT(T.ce[:, 0:128], T.psx[:, 2 * wx - 128:2 * wx], T.ha[:, 64:192], OP.add, tok["X8"])
        if n == "ceY":
            return TT(T.ce[:, 128:256], cb["Y"], T.ha[:, 192:320], OP.add, tok["Y8"])
        if n[0] == "m" and NB == 2:
            return TT(T.xi[:, c], out_of(1, j), T.mt[:, c], OP.min, tok["U%d" % j], tok["M%d" % j])
        if n[0] in "mM":
            return TT((T.xi if n[0] == "m" else T.mt)[:, c], out_of(0, j), T.ce[:, c], OP.min, tok["T%d" % j], tok["ce" + "XY"[j // 2]])
        if n[0] == "a":
            return TS(T.ai[:, c], T.xi[:, c], M - 1, OP.bitwise_and, None, None, tok["m%d" % j])
        if n[0] == "c":
            return TT(cand(j), q4, T.ai[:, c], OP.add, tok["a%d" % j])
        if n[0] == "i":
            return TS(T.l2[:, c], cand(j), 0.5, OP.mult, -0.25, OP.add, tok["c%d" % j])
        if n[0] == "d" and "z2" in P_ORDER:
            toks(("i0", "d0", "d0")[j])
        if n in ("d0", "d1") and "z2" in P_ORDER:
            return TT(steps[:, 2 - j::4], cand(j + 1), cand(j), OP.subtract, *toks("c%d" % j, "c%d" % (j + 1)))
        if n == "z1":
            tok["z0"] = FILL(T.sf[:, 0::4], 0)
            return tok["z0"]
        if n[0] == "b":
            return TS(T.ah[:, c], T.xi[:, c], 1, OP.bitwise_and, None, None, tok["m%d" % j])
        if n[0] == "w":
            return TS(T.mh[:, c], T.ah[:, c], -15.0, OP.mult, 16.0, OP.add, tok["b%d" % j])
        if n[0] == "d":
            out = steps[:, 2 - j::4] if whole else T.psv[:, c]
            return TT(out, T.ai[:, 64 * j + 64:64 * j + 128], T.ai[:, c], OP.subtract, *toks("a%d" % j, "a%d" % (j + 1)))
        if n[0] == "n":
            return TT(T.vi[:, c], T["ps%d" % j][:, 384:448], T.mh[:, c], OP.mult, tok["H%d" % j], tok["w%d" % j])
        if n == "z0":
            if whole:
                CP(steps[:, 3::4], T.cc[:, 0:64], tok["c0"])
                return FILL(T.sf[:, 0::4], 0)
            return FILL(T.sf[:, 0:128:2], 0)
        if n == "scan":
            return SCAN(T.so[:, :], T.sf[:, :], steps, *toks("s0", "s1", "s2", "z0", "d0", "d1", "d2", "c0"))
        if n == "fma":
            return SCAN(T.so[:, 0:128], T.sf[:, 0:128], T.psv[:, 256:384], *toks("s2", "z0", "keep", "rest"))
        if n[0] == "s":
            out = T.sf[:, 3 - j::4] if whole else T.sf[:, 1:128:2] if last and j == 2 else T.vb[:, c]
            return TS(out, T.vi[:, c], 4 + rank, OP.arith_shift_right, 1, OP.bitwise_and, tok["n%d" % j])
        if n == "u0":
            return TT(T.uu[:, 0:64], T.psv[:, 0:64], T.vb[:, 0:64], OP.mult, tok["s0"], tok["d0"])
        if n == "first":
            return TT(first, T.uu[:, 0:64], T.cc[:, 0:64], OP.add, tok["u0"], tok["c0"])
        if n[0] == "y":
            return TT(T.psv[:, 320 + 64 * j:384 + 64 * j], T.psv[:, c], T.vb[:, 0:64], OP.mult, tok["s0"], tok["d%d" % j])
        if n == "u1":
            return TT(T.uu[:, 64:128], T.psv[:, 384:448], T.vb[:, 64:128], OP.mult, tok["s1"], tok["y1"])
        if n == "rest":
            return TT(rest, T.psv[:, 448:512], T.vb[:, 64:128], OP.mult, tok["s1"], tok["y2"])
        if n == "keep":
            return TT(keep, first, T.uu[:, 64:128], OP.add, tok["u1"], tok["first"])
        if n == "u2":
            return TT(T.uu[:, 128:192], rest, T.vb[:, 128:192], OP.mult, tok["s2"], tok["rest"])
        if whole or last:
            res = T.so[:, 3::4] if whole else T.so[:, 1:128:2]
            return CP(T.xx[:, :] if n == "x" else T.l3[:, :], res, tok["scan" if whole else "fma"])
        if n == "x":
            return TT(T.xx[:, :], keep, T.uu[:, 128:192], OP.add, tok["u2"], tok["keep"])
        return CP(T.l3[:, :], T.xx[:, :], tok["x"])

    def aop(n):
        if n[0] in "fyc":
            return sop(n, "a")
        if ":" in n:
            return look("a", n)
        if n[0] in "XY":
            return hash_step(n[0], n[1])
        if n == "x":
            return COPY(T.xx[:, :], T.so[:, 3::4] if whole else T.so[:, 1:128:2], 1.0, tok["scan" if whole else "fma"])
        if n[0] == "k" and len(n) == 3:
            return table("a", n)
        if n == "k2":
            return COPY(T.ft[:, 0:256], pk, 1.0, tok["k1"])
        if n == "k4":
            return COPY(T.ft[:, 256:512], rp, 1.0, tok["k3"])
        if n == "id4":
            return COPY(T.id4k[:, :], T.idt[:, :], float(M), t_id)
        if n == "id16":
            return COPY(T.id16[:, :], T.idt[:, :], 16.0, t_id)
        j = int(n[1])
        x0, x1, grp = PP[j]
        return COPY(T.sw[:, H * rank + x0:H * rank + x1], T["ps%d" % j][:, 0:x1 - x0], 1.0, tok["p%d" % j])

    def top(n):
        if n[0] in "XY":
            return hash_step(n[0], n[1])
        if n == "psr":
            return done("t", group(T.psr[:, 0:11], [(T.gs[:, :], T.rkf[:, 0:11])], *toks("r0", "r1", "gs")))
        if n == "q4":
            return done("t", group(q4, [(T.id4k[:, :], T.og[:, 64 * j:64 * j + 64]) for j in range(7)],
                                   max(toks(*["g%d" % j for j in range(7)])), tok["id4"]))
        i = int(n[1])
        ps = T["ps%d" % i]
        if n[0] == "p":
            x0, x1 = bs + 2 * PP[i][0], bs + 2 * PP[i][1]
            ins = group(ps[:, 0:(x1 - x0) // 2], [(T.idt[:, :], T.fw[:, x0:x1:2]), (T.id16[:, :], T.fw[:, x0 + 1:x1:2])],
                        tok[["ls%d" % j for j, (y0, y1) in enumerate(SP) if y0 <= PP[i][0] < y1][0]], t_id, tok["id16"],
                        *(toks("k5b") if i == 3 and "k0a" in V_ORDER else []))
        elif n[0] == "H":
            ins = group(ps[:, 384:448], [(T.cm[:, 127 * u:127 * u + 128], T["gb%d" % i][:, u::16]) for u in range(16)],
                        tok["con"], *tok["g" + n])
        else:
            h = "TU".index(n[0])
            free = toks(*moved) if h == 0 else toks("ceX", "ceY") if i < 2 else toks("m%d" % (i - 2))
            far = [(T.id4k[:, :], T.pen[:, 64 * h:64 * h + 64])] if NB == 2 else []
            ins = group(out_of(h, i), far +
                        [(T.c0[:, 128 * h + 15 - u:128 * h + 143 - u], T["ga%d" % i][:, u::16]) for u in range(16)],
                        tok["wt%d" % h], *(tok["gT%d" % i] + free + (toks("q%d" % h) if far else [])))
        return done("t", ins)

    lr = [0]

    def send(dsts, x, sem, out, *deps):
        need("p", deps)
        lr[0] += spread(g, T, topo, core, dsts, x, sem, out)
        return ("lr", lr[0])

    def pop(n):
        if ":" in n:
            return look("p", n)
        if n == "gs":
            return SEL(T.gs[:, :], T.f8[:, :], [[-1, 8], [0, 16]], OP.is_equal, 0, 1, t_f8)
        if n == "z2":
            tok["z0"] = done("p", g.iota(T.sf[:, 0::4], [[0, 64]], 0, 0))
            return tok["z0"]
        if n == "kc":
            CONST(T.kc[:, 0:4], [[M, 4]], 0)
            return CONST(T.kc[:, 4:8], [[-1, 4]], 0)
        if n[:2] == "wt":
            h = int(n[2])
            w = T.c0[:, 128 * h + 15:128 * h + 143:16]
            x = SEL(w, T.on[:, 0:8], [[-16, 8]], OP.is_ge, -3 * h, 1, t_w0)
            return SEL(w, w, [[16, 8]], OP.is_ge, 3 * h + 2, -1, x)
        nh = 4 // NB
        w = T.c0[:, 15:15 + 128 * nh:16]
        if n == "wa":
            return SEL(w, T.on[:, 0:8 * nh], [[-3, nh], [-16, 8]], OP.is_ge, 0, 1, t_w0)
        if n == "wb":
            tok["wt0"] = tok["wt1"] = SEL(w, w, [[3, nh], [16, 8]], OP.is_ge, 2, -1, tok["wa"])
            return tok["wt0"]
        if n == "con":
            return SEL(T.cm[:, 0:2048:16], T.on[:, :], [[-1, 16], [-16, 8]], OP.is_equal, 0, 1, *tok["zeros"])
        if n == "hold":
            return need("p", [("aft%d" % T.rank_of(c), 3 * len(topo.engines(c, core))) for c in others])
        if n[0] == "@":
            return need("p", toks(n[1:]))
        j = int(n[1])
        out, sem, way = piece(T, rank, n)
        if n[0] == "t":
            x, deps = T.ft[:, 256 * j:256 * j + 256], made_k((2, 4, 5)[j])
        else:
            x, deps = out, toks(*["e%d" % i for i in range(len(PP)) if PP[i][2] == j]) if n[0] == "h" else toks("lv%d" % j)
        if way == "s":
            return send(others[::-1] if n[0] == "t" and not SYM else others, x, sem, out, *deps)
        if way == "n":
            return send([hc], x, n, out, *deps)
        send([helper_of(across(core, T, topo), T, topo)], x, n, out, *deps)
        return send([c for c in others if topo.die(c) == topo.die(core)], x, sem, out)

    def sop(n, dq="s"):
        if n == "chosen":
            return dma(dq, T.chosen[:, :], T.xx[:, :], "st", tok["x"])
        if n[0] == "y":
            c0, c1 = [int(c) for c in n.split(":")[1:]]
            deps = toks(*[m for m in V_ORDER + A_ORDER if m[:2] == "V0" and c0 <= int(m.split(":")[1]) < c1])
            return dma(dq, T.y[:, 16 * c0:16 * c1], T.yt[:, 16 * c0:16 * c1], "st", *deps)
        if n[0] == "F":
            return look("s", n)
        if n[0] == "@":
            return need("s", toks(n[1:]))
        k = int(n[1])
        if n[0] == "v":
            return s_vec(k)
        if n[0] == "s":
            return s_seen(k)
        q = owners[k]
        deps = made_k(2) + made_k(4) + made_k(5) if k == 0 else [("aft%d" % q, 3 * len(topo.engines(T.cores[q], core)))]
        blk = (q % NB - bs // M) % NB if NB == 2 else k
        deps += tok["full%d" % blk] if blk else toks(*packed)
        if part and blk == NB - 1:
            deps += tok["src"]
        for f in range(3):
            x = dma(dq, T.fw[3 * (q // NB) + f::16, M * (q % NB):M * (q % NB) + M],
                    T.ft[:, 256 * f:256 * f + 256] if k == 0 else T.fl[3 * q + f], "fx", *deps)
        return x

    queues = [(list(V_ORDER), vop), (list(A_ORDER), aop), (list(T_ORDER), top), (list(P_ORDER), pop), (list(S_ORDER), sop)]
    while any([x for x, f in queues]):
        made = 0
        for x, f in queues:
            while x:
                try:
                    r = f(x[0])
                except KeyError:
                    break
                if r is not None:
                    tok[x[0]] = r
                made += 1
                if x.pop(0)[0] == "F":
                    break
        assert made

    need("p", [("lr", lr[0])])
    need("s", [(s, cnt[s]) for s in cnt])
